import numpy as np, ml_dtypes
CORES = [35,38,43,46]
N = 4
BF = ml_dtypes.bfloat16
def gentries(a):
    return np.ascontiguousarray(a.reshape(8, 16, -1).transpose(0, 2, 1)).reshape(8, -1)
def gtable(e):
    e = np.asarray(e); return np.ascontiguousarray(e.reshape(8, -1, 16).transpose(0, 2, 1)).reshape(128, -1).astype(np.int32)
W, L, B, VI, PS, ST = 4096, 16, 256, 4, 1, 16
KAP = 241 * np.arange(L) + 37
def tables_of(rng):
    lv = rng.random((N, 8, 16, W), dtype=np.float32); x = rng.integers(0, 16, (N, 8, 16, W))
    h = rng.choice(np.array([0.15, 0.22, 0.3]), (N, 8, 1, 1)); w = rng.choice(np.array([0.12, 0.18]), (N, 8, 1, 1))
    e = np.where(lv < h, 12 + (x & 3), np.where(lv < h + w, x & 3, 4 + (x & 7)))
    nd = rng.choice(np.array([0.0, 0.05, 0.1, 0.2]), (N, 8, 1, W)); x = rng.integers(0, 12, (N, 8, 16, W))
    return e, np.where(rng.random((N, 8, 16, W), dtype=np.float32) < nd, 12 + (x & 3), x)
def own_steps(rng, s):
    return np.take_along_axis(s, rng.integers(0, L, (N, 8, L, B)), axis=2)
def pack(e, p, s, q, st, th):
    return {"eff": e.reshape(N, 128, W).astype(np.float32).astype(BF), "req": p.reshape(N, 128, W).astype(np.float32).astype(BF),
            "act": np.stack([gtable(a.reshape(8, L * B)) for a in s]), "why": np.stack([gtable(a.reshape(8, L * B)) for a in q]),
            "st0": np.ascontiguousarray(st).reshape(N, 128, B).astype(np.float32).astype(BF), "bar": np.stack([gtable(a) for a in th])}
def setup_inputs(rng):
    e, p = tables_of(rng); s = rng.integers(0, W, (N, 8, L, B)); w = rng.integers(0, 5, (N, 8, L, B))
    q = np.where(w < 2, -1, np.where(w < 4, own_steps(rng, s), rng.integers(0, W, (N, 8, L, B))))
    return pack(e, p, s, q, rng.integers(0, 16, (N, 8, 16, B)), rng.choice(np.array([0, 1, 2, 2, 3, 3, 4]), (N, 8, B)))
def setup_inputs_alike(rng):
    e, p = tables_of(rng)
    fw = np.concatenate([np.argsort(rng.random((N, 8, W - 2)), axis=-1)[..., :4] + 1, np.zeros((N, 8, 1), np.int64), np.full((N, 8, 1), W - 1)], axis=2)
    ix = np.broadcast_to(fw[:, :, None, :], (N, 8, 16, 6))
    np.put_along_axis(e, ix, rng.choice(np.array([0, 3, 4, 8, 11, 12, 15]), (N, 8, 16, 6)), axis=3)
    np.put_along_axis(p, ix, np.where(rng.random((N, 8, 16, 6)) < 0.2, 12, 11), axis=3)
    n = rng.integers(0, 6, (N, 8, L, B)); n[:, 1::2] = n[:, 1::2, :, :1]
    n = np.where(rng.random((N, 8, 1, B)) < 0.15, n[:, :, :1], n)
    s = np.take_along_axis(fw, n.reshape(N, 8, L * B), axis=2).reshape(N, 8, L, B)
    q = np.take_along_axis(fw, rng.integers(0, 6, (N, 8, L * B)), axis=2).reshape(N, 8, L, B)
    q = np.where(rng.random((N, 8, L, B)) < 0.4, -1, q)
    return pack(e, p, s, q, rng.integers(0, 16, (N, 8, 16, B)), rng.integers(0, 5, (N, 8, B)))
def setup_inputs_corners(rng):
    o = np.argsort(rng.random((N, 8, W)), axis=-1); kc = np.zeros((N, 8, W), np.int64)
    np.put_along_axis(kc, o, np.broadcast_to(np.arange(W) & 7, (N, 8, W)), axis=2)
    k4 = kc[:, :, None, :]; bit = rng.integers(0, 2, (N, 8, 16, W)) == 1
    e = np.where(bit, np.array([4, 0, 12, 4, 4, 4, 4, 4])[k4], np.array([11, 3, 15, 11, 11, 11, 11, 11])[k4])
    e = np.where(k4 == 7, np.array([3, 4, 11, 12])[rng.integers(0, 4, (N, 8, 16, W))], e)
    rk = ((2 * rng.integers(0, 8, (N, 8, 1, W)) + 1) * np.arange(16)[None, None, :, None] + rng.integers(0, 16, (N, 8, 1, W))) & 15
    nd = np.where(k4 == 7, rng.integers(0, 4, (N, 8, 1, W)), np.array([0, 0, 0, 1, 2, 3, 16, 0])[k4]); bit = rng.integers(0, 2, (N, 8, 16, W)) == 1
    p = np.where(rk < nd, np.where(bit, 12, 15), np.where(bit, 11, 0))
    tp = rng.integers(0, 8, (N, 8, 1, B)); y = rng.integers(4, 7, (N, 8, 1, B)); v = rng.integers(1, L, (N, 8, 1, B)); kk = np.arange(L)[None, None, :, None]
    j = rng.choice(np.array([0, L // 2, L - 2]), (N, 8, 1, B)); cp = np.zeros((N, 8, L, B), np.int64)
    cp = np.where((tp == 1) & (kk == 0), y, cp)
    cp = np.where((tp == 2) & (kk == j), 1, cp); cp = np.where((tp == 2) & (kk == L - 1), y, cp)
    cp = np.where(tp == 3, 3, cp)
    for a, b in ((L // 3, 4), (L // 2, 5), (L - 1, 6)): cp = np.where((tp == 4) & (kk == a), b, cp)
    cp = np.where(tp == 5, np.where(kk == v, y, 1), cp)
    cp = np.where((tp == 6) & (kk == 0), 2, cp); cp = np.where((tp == 6) & (kk == L - 1), 1, cp)
    cp = np.where(tp == 7, rng.integers(0, 8, (N, 8, L, B)), cp)
    s = np.take_along_axis(o, (8 * rng.integers(0, W // 8, (N, 8, L, B)) + cp).reshape(N, 8, L * B), axis=2).reshape(N, 8, L, B)
    st = np.array([7, 8, 0, 15])[rng.integers(0, 4, (N, 8, 16, B))]
    st = np.where((tp == 1) | (tp == 3) | (tp == 4), 7, np.where(tp == 2, 8, st))
    h = np.where(tp == 2, j, np.where(tp == 5, v - 1, np.where(tp == 4, L // 3, 0))); own = np.take_along_axis(s, h, axis=2)
    qm = rng.integers(0, 4, (N, 8, 1, B))
    q = np.where(qm == 0, -1, np.where(qm == 1, own, np.where(qm == 2, np.where(rng.random((N, 8, L, B)) < 0.5, own, -1), own_steps(rng, s))))
    return pack(e, p, s, q, st, rng.choice(np.array([0, 1, 2, 3, 16]), (N, 8, B)))
def setup_inputs_ends(rng):
    t = W - 1
    e = 15 * (rng.random((N, 8, 16, W), dtype=np.float32) < rng.choice(np.array([0.0, 0.1, 0.5, 0.9, 1.0]), (N, 8, 1, W))).astype(np.int64)
    p = 15 * (rng.random((N, 8, 16, W), dtype=np.float32) < rng.choice(np.array([0.0, 0.0, 0.1, 0.3, 1.0]), (N, 8, 1, W))).astype(np.int64)
    kk = np.arange(L)[None, None, :, None]; x = rng.choice(np.array([0, 1, L // 2, L - 2, L - 1, L]), (N, 8, 1, B)); x[..., B - 1] = L - 2; x[..., B - 2] = L - 1
    m = rng.random((N, 8, 1, B)) < 0.6; m[..., B - 2:] = True
    s = t * np.where(m, (kk >= x).astype(np.int64), rng.integers(0, 2, (N, 8, L, B)))
    q = np.where(rng.random((N, 8, L, B)) < rng.choice(np.array([0.0, 0.2, 0.5, 1.0]), (N, 8, 1, B)), t, -1)
    st = 15 * (rng.random((N, 8, 16, B)) < rng.choice(np.array([0.0, 0.5, 1.0]), (N, 8, 1, B))).astype(np.int64)
    th = 16 * rng.integers(0, 2, (N, 8, B)); th[..., B - 1] = 16; th[..., B - 2] = 0
    c0 = (KAP * t) & t; c1 = ((t * t >> 5) + KAP * t) & t
    for r in range(N):
        for g in range(8):
            k = (N + 7 - r - g) & 3; u = e[r, g]
            if k == 3: continue
            if k == 0:
                u[0, c0] = 0; u[:, c0[L - 1]] = 15; u[:, 0] = 0; u[:, t] = 15 * rng.integers(0, 2, 16)
            elif k == 1:
                u[:, c1[[1, 2, L - 1]]] = 15; u[5, c1[0]] = 0; u[:, 0] = 15; u[:, t] = 0
            else:
                u[:, c1] = 0; u[:, 0] = 15; u[:, t] = 15; u[rng.permutation(16)[:2], t] = 0
            p[r, g, :, 0] = 0; p[r, g, :, t] = 15
    return pack(e, p, s, q, st, th)
def setup_inputs_full(rng):
    e, p = tables_of(rng); s = rng.integers(0, W, (N, 8, L, B)); st = rng.integers(0, 16, (N, 8, 16, B)); th = rng.choice(np.array([0, 1, 2, 2, 3, 3, 4]), (N, 8, B)); kk = np.arange(L)[:, None]
    for r in range(N):
        for g in range(8):
            m = (g + r + 2 - N) & 7
            if m > 4: continue
            o = rng.permutation(W).reshape(32, W // 32); kc = np.zeros(W, np.int64); kc[o] = np.arange(32)[:, None]
            y = rng.integers(0, 4, (16, W)); e[r, g] = np.where(kc < 17, rng.integers(4, 12, (16, W)), np.where(kc < 20, y, 12 + y))
            rk = ((2 * rng.integers(0, 8, W) + 1) * np.arange(16)[:, None] + rng.integers(0, 16, W)) & 15
            p[r, g] = np.where((rk < kc) & (kc < 17), rng.integers(12, 16, (16, W)), rng.integers(0, 12, (16, W)))
            n = rng.integers(2, 16, B) if m == 0 else rng.integers(4, 17, B)
            x = rng.choice(np.array([0, L // 2, L - 1, L - 1]), B); j = rng.integers(0, L, B); low = (j < x) & (rng.random(B) < 0.5)
            calm = rng.random(B) < (0.1 if m else 0.0)
            if m: calm[B // 2] = True
            kd = np.where(kk == x, n, np.where(kk > x, rng.integers(0, 32, (L, B)), 0)); kd = np.where((kk == j) & low, rng.integers(17, 20, B), kd); kd = np.where(calm, 0, kd)
            s[r, g] = o[kd, rng.integers(0, W // 32, (L, B))]
            st[r, g] = rng.integers(0, 8, (16, B)) + 8 * (low | calm).astype(np.int64)
            up = np.ones(B, np.int64) if m == 0 else rng.integers(0, 2, B)
            th[r, g] = np.minimum(n + up, 16)
    w = rng.integers(0, 5, (N, 8, L, B))
    q = np.where(w < 2, -1, np.where(w < 4, own_steps(rng, s), rng.integers(0, W, (N, 8, L, B))))
    return pack(e, p, s, q, st, th)
def setup_inputs_spread(rng):
    def power(hi, pw, shape): return np.minimum((hi * rng.random(shape, dtype=np.float32) ** pw.astype(np.float32)).astype(np.int64), hi - 1)
    e = power(16, rng.choice(np.array([0.5, 1.0, 2.0]), (N, 8, 16, 1)), (N, 8, 16, W))
    p = power(16, rng.choice(np.array([1.0, 3.0, 8.0, 20.0, 20.0]), (N, 8, 1, W)), (N, 8, 16, W))
    s = power(W, rng.choice(np.array([0.25, 1.0, 4.0]), (N, 8, L, 1)), (N, 8, L, B))
    q = np.where(rng.random((N, 8, L, B)) < 0.5, own_steps(rng, s), rng.integers(-1, W, (N, 8, L, B)))
    return pack(e, p, s, q, power(16, rng.choice(np.array([0.3, 1.0, 3.0]), (N, 8, 1, B)), (N, 8, 16, B)), power(17, rng.choice(np.array([1.0, 3.0, 6.0]), (N, 8, 1)), (N, 8, B)))
def check_inputs(d):
    bad = []
    for k, lo, hi in (("eff", 0, 15), ("req", 0, 15), ("act", 0, W - 1), ("why", -1, W - 1), ("st0", 0, 15), ("bar", 0, 16)):
        v = np.asarray(d[k]).astype(np.float64)
        if not (np.min(v) >= lo and np.max(v) <= hi): bad.append("range of " + k)
        elif np.any(v != np.floor(v)): bad.append("whole numbers in " + k)
    return bad
def pick(tab, ix):
    return np.stack([tab[g][:, ix[g]] for g in range(8)])
def visit(E, P, S, Q, s, th, R, t):
    kk = np.arange(L)[None, :, None]
    es = pick(E, S.reshape(8, L * B)).reshape(8, 16, L, B); ps = pick(P, S.reshape(8, L * B)).reshape(8, 16, L, B)
    flaw = np.zeros((8, 16, L, B), bool)
    for k in range(L):
        flaw[:, :, k] = (ps[:, :, k] >= 12) & (s < 8)
        s = np.where((es[:, :, k] >= 12) | (es[:, :, k] <= 3), es[:, :, k], s)
    over = np.add.reduce(flaw.astype(np.int16), axis=1) >= 2 + (R & 1)
    found = np.any(over, axis=1); ks = np.argmax(over, axis=1)
    fl = np.take_along_axis(flaw, ks[:, None, None, :], 2); need = np.take_along_axis(ps, ks[:, None, None, :], 2) >= 12
    low = np.any((es <= 3) & fl, axis=1) & (kk < ks[:, None, :])
    d = np.where(np.any(low, axis=1), L - 1 - np.argmax(low[:, ::-1], axis=1), ks)
    a = np.take_along_axis(S, ks[:, None, :], 1); z = np.take_along_axis(S, d[:, None, :], 1)
    c = ((a * z >> 5) + KAP[None, :, None] * a + 97 * t) & (W - 1)
    ec = pick(E, c.reshape(8, L * B)).reshape(8, 16, L, B)
    score = np.add.reduce(((ec >= 12) & fl).astype(np.int64), axis=1) - np.add.reduce(((ec <= 3) & need & ~fl).astype(np.int64), axis=1)
    m = np.argmax(score, axis=1); best = np.max(score, axis=1); cm = np.take_along_axis(c, m[:, None, :], 1)
    put = (found & (best >= th))[:, None, :]; ret = (found & (best < th))[:, None, :]
    kb = ks[:, None, :]
    si = np.where(kk < kb, S, np.where(kk == kb, cm, np.concatenate([S[:, :1], S[:, :-1]], axis=1)))
    qi = np.where(kk < kb, Q, np.where(kk == kb, z, np.concatenate([Q[:, :1], Q[:, :-1]], axis=1)))
    go = (kk == d[:, None, :]) | (Q == z)
    order = np.argsort(go, axis=1, kind="stable"); kept = kk < L - np.add.reduce(go.astype(np.int64), axis=1)[:, None, :]
    sr = np.where(kept, np.take_along_axis(S, order, 1), c); qr = np.where(kept, np.take_along_axis(Q, order, 1), -1)
    at = ST * np.arange(B)[None, :] + (np.add.reduce(s.astype(np.int64), axis=1) & (ST - 1))
    e2 = np.array(E); np.put_along_axis(e2, np.broadcast_to(at[:, None, :], (8, 16, B)), (pick(E, at) + s) >> 1, axis=2)
    return np.where(put, si, np.where(ret, sr, S)), np.where(put, qi, np.where(ret, qr, Q)), s, e2, int(np.count_nonzero(ret))
def reference(eff, req, act, why, st0, bar):
    E = [x.astype(np.float32).astype(np.int16).reshape(8, 16, W) for x in eff]; P = [x.astype(np.float32).astype(np.int16).reshape(8, 16, W) for x in req]
    S = [gentries(x).astype(np.int64).reshape(8, L, B) for x in act]; Q = [gentries(x).astype(np.int64).reshape(8, L, B) for x in why]
    s = [x.astype(np.float32).astype(np.int16).reshape(8, 16, B) for x in st0]; th = [gentries(x).astype(np.int64) for x in bar]; R = [0] * N
    for t in range(VI):
        v = [visit(E[r], P[r], S[r], Q[r], s[r], th[r], R[r], t) for r in range(N)]
        E = [x[3] for x in v]; R = [x[4] for x in v]; go = PS if t < VI - 1 else 0
        S = [v[(r - go) % N][0] for r in range(N)]; Q = [v[(r - go) % N][1] for r in range(N)]; s = [v[(r - 1) % N][2] for r in range(N)]
    return {"ys": np.stack([gtable(x.reshape(8, L * B)) for x in S]).astype(np.float32), "yw": np.stack([gtable(x.reshape(8, L * B)) for x in Q]).astype(np.float32),
            "ye": np.stack([x.reshape(128, W) for x in E]).astype(np.float32).astype(BF)}

@@ -1,0 +1,643 @@
+import numpy as np
+import math
+import comms_topo
+from concourse.mybir import AluOpType as A, ActivationFunctionType as F
+
+NCH, W, L, VI = 2, 4096, 16, 4
+LC = 256 // NCH
+CA = LC * L
+NJ = LC // 16
+MACT = 4
+LN2 = math.log(2.0)
+BIG = 1024.0
+NDMA = 80
+
+SCRATCH = {}
+SEMAPHORES = ["qv", "qa", "qt", "qg"] + ["d%d" % i for i in range(NDMA)]
+for _t in range(VI - 1):
+    for _c in range(NCH):
+        SEMAPHORES += ["ap%d_%d" % (_t, _c), "as%d_%d" % (_t, _c), "lp%d_%d" % (_t, _c), "ls%d_%d" % (_t, _c)]
+
+
+LOG = {}
+_SHORT = {"bfloat16": "bf", "float16": "hf", "float32": "ff", "int32": "nn", "uint16": "uu"}
+
+
+def _buf(name, cols, dtype, where="sbuf"):
+    if where == "psum":
+        SCRATCH[name] = (where, [128, cols], dtype)
+        LOG[name] = (where, cols, dtype, name, 0)
+        return
+    t = "pk" + _SHORT[dtype]
+    o = SCRATCH[t][1][1] if t in SCRATCH else 0
+    SCRATCH[t] = ("sbuf", [128, o + -(-cols // 64) * 64], dtype)
+    LOG[name] = (where, cols, dtype, t, o)
+
+
+for _n in ("er", "gt", "nt", "tq"):
+    _buf(_n, W, "bfloat16")
+for _n in ("ip", "ic", "gp", "gc", "kp", "kc"):
+    _buf(_n, 128, "int32")
+for _n in ("dd", "cc", "pp", "ns", "eye", "blk", "str", "tri", "first", "half", "shd", "sh1", "sh2", "sh4", "sh8", "neg",
+           "i4", "im85", "i85", "i512", "i143", "i18", "i2048", "mt", "mth", "mr", "blkz", "mag", "ones", "nblk"):
+    _buf(_n, 128, "bfloat16")
+for _n in ("wk", "kw", "br", "wh"):
+    _buf(_n, 16 * 128, "bfloat16")
+_buf("thf", 128, "float32")
+_buf("allo", 128, "float32")
+for _n in ("kcol", "kap", "cq", "k16", "pb", "thr", "m1c"):
+    _buf(_n, 8, "float32")
+_buf("rci", 8, "int32")
+_buf("xbase", NJ, "bfloat16")
+_buf("xbi", NJ, "int32")
+_buf("barl", 16, "int32")
+_buf("barb", 16, "bfloat16")
+_buf("bark", 256, "bfloat16")
+_buf("actk", 256, "int32")
+_buf("whyk", 256, "int32")
+_buf("sti", 256, "bfloat16")
+_buf("sth", 256, "bfloat16")
+_buf("stc", 256, "bfloat16")
+_buf("ysk", 256, "float32")
+_buf("ywk", 256, "float32")
+for _c in range(NCH):
+    for _t in range(VI):
+        _buf("w%d_%d" % (_t, _c), 256 * LC // 128, "float16")
+        _buf("wo%d_%d" % (_t, _c), 256 * LC // 128, "float16")
+        _buf("s%d_%d" % (_t, _c), LC, "bfloat16")
+        _buf("so%d_%d" % (_t, _c), LC, "bfloat16")
+        _buf("ac%d_%d" % (_t, _c), 8, "float32")
+    _buf("gb%d" % _c, CA + 16, "bfloat16")
+    for _n in ("kb", "zb", "fl", "cg", "hb"):
+        _buf("%s%d" % (_n, _c), CA, "bfloat16")
+    for _n in ("e15", "k15", "t15", "val", "h8", "ov", "X", "zx", "nx", "hx", "w8", "f1", "T", "D", "pw", "eq", "M", "insi",
+               "mi", "xi", "ret", "qe", "go", "fm", "rb", "ar", "eo", "ne", "cl", "hh", "ng"):
+        _buf("%s_%d" % (_n, _c), LC, "bfloat16")
+    for _n in ("xs", "ds", "cf", "mc"):
+        _buf("%s_%d" % (_n, _c), LC, "float16")
+    for _n in ("a1", "a2", "m0", "m1", "m2", "m3", "wb", "iv", "fi"):
+        _buf("%s_%d" % (_n, _c), 2 * LC, "float16")
+    for _n in ("f4", "y7", "pr", "sh", "sm", "ci", "ri", "mk", "es", "eh"):
+        _buf("%s_%d" % (_n, _c), LC, "int32")
+    for _n in ("tj", "sx", "tb"):
+        _buf("%s_%d" % (_n, _c), LC, "float32")
+    for _n in ("off", "c16"):
+        _buf("%s_%d" % (_n, _c), LC, "uint16")
+    for _n in ("xl", "sl", "vl"):
+        _buf("%s_%d" % (_n, _c), max(NJ, 2), "uint16")
+    for _n in ("ui", "uj", "uk", "vb"):
+        _buf("%s_%d" % (_n, _c), NJ, "int32")
+NB = 8 // NCH
+for _i in range(8):
+    _buf("p%d" % _i, 512, "float32", "psum")
+
+
+def overlap(a, b):
+    if a[0] != b[0] or a[1] >= b[2] or b[1] >= a[2]:
+        return False
+    if a[3] == b[3] and a[3] > 1 and (a[1] - b[1]) % a[3]:
+        return False
+    if a[4] is not None and b[4] is not None and a[4] != b[4]:
+        return False
+    return True
+
+
+def rank_program(g, core, T, topo):
+    rank = T.rank_of(core)
+    if rank is None:
+        return
+    nxt = T.cores[(rank + 1) % len(T.cores)]
+    ops = []
+    acc = {}
+    Q = {"v": g.vector, "a": g.scalar, "t": g.tensor, "g": g, "s": g.sync}
+    QS = {"v": "qv", "a": "qa", "t": "qt", "g": "qg"}
+    dn = [0]
+
+    def R(name, a=None, b=None, st=1, p=None):
+        n = LOG[name][1] if name in LOG else T[name].shape[1]
+        return (name, 0 if a is None else a, n if b is None else b, st, p)
+
+    def ap(r):
+        t, o = (LOG[r[0]][3], LOG[r[0]][4]) if r[0] in LOG else (r[0], 0)
+        if r[4] is not None:
+            return T[t][r[4][0]:r[4][1]:r[4][2], o + r[1]:o + r[2]]
+        if r[3] > 1:
+            return T[t][:, o + r[1]:o + r[2]:r[3]]
+        return T[t][:, o + r[1]:o + r[2]]
+
+    def ind(win, off):
+        return ("IND", win, off)
+
+    def x(r):
+        if isinstance(r, tuple):
+            if r[0] == "IND":
+                return ap(r[1]).indirect(ap(r[2]))
+            return ap(r)
+        return r
+
+    def n_of(r):
+        return -(-(r[2] - r[1]) // r[3])
+
+    def add(q, fns, reads, writes, cost, kind="c", lat=0.0, sem=None, inc=0, extra=()):
+        i = len(ops)
+        rd = []
+        for r in reads:
+            if isinstance(r, tuple):
+                rd += [r[1], r[2]] if r[0] == "IND" else [r]
+        wr = []
+        for r in writes:
+            if r[0] == "IND":
+                wr.append(r[1])
+                rd.append(r[2])
+            else:
+                wr.append(r)
+        deps = set(extra)
+        for lst, isw in ((rd, False), (wr, True)):
+            for r in lst:
+                ps = r[0] in PS
+                for (j, r2, w2) in acc.get(r[0], ()):
+                    if j == i:
+                        continue
+                    if ps and ops[j]["q"] != q:
+                        deps.add(j)
+                    elif (isw or w2) and overlap(r, r2):
+                        deps.add(j)
+        for lst, isw in ((rd, False), (wr, True)):
+            for r in lst:
+                cur = acc.setdefault(r[0], [])
+                ps = r[0] in PS
+                if isw and r[3] == 1 and r[4] is None and not ps:
+                    cur[:] = [e for e in cur if not (e[1][1] >= r[1] and e[1][2] <= r[2])]
+                cur.append((i, r, isw))
+                if ps and isw:
+                    cur[:] = [e for e in cur if e[0] >= i - 1500]
+        ops.append({"q": q, "fns": fns, "deps": deps, "cost": cost, "kind": kind, "lat": lat, "sem": sem, "inc": inc})
+        return i
+
+    def two(*rs):
+        return all(isinstance(r, tuple) and r[0] in LOG and LOG[r[0]][2] in ("bfloat16", "float16", "uint16") and r[0] not in PS for r in rs)
+
+    CY = 0.00105
+
+    def vc(n, rate):
+        return 0.05 + max(64, n * rate) * CY
+
+    def tt(out, a, b, op):
+        i = a[0] == "IND"
+        rate = 1.6 if i or out[0] == "IND" else (1.0 if (a[0][0] == "p" and a[0] in PS) or (b[0] in PS) else 2.0)
+        return add("v", [lambda: g.vector.tensor_tensor(x(out), x(a), x(b), op)], [a, b], [out], vc(n_of(out), rate))
+
+    def ts(out, a, s1, op0, s2=None, op1=None):
+        rate = 0.5 if two(out, a) else 1.0
+        if op1 is None:
+            f = lambda: g.vector.tensor_scalar(x(out), x(a), x(s1), None, op0)
+        else:
+            f = lambda: g.vector.tensor_scalar(x(out), x(a), x(s1), x(s2), op0, op1)
+        return add("v", [f], [a, s1, s2], [out], vc(n_of(out), rate))
+
+    def cp(out, a):
+        sc = out[0] == "IND"
+        rate = 4.0 if sc else (0.5 if two(out, a) else 1.0)
+        return add("v", [lambda: g.vector.tensor_copy(x(out), x(a))], [a], [out], vc(n_of(a), rate))
+
+    def act(out, a, func, bias=None, scale=None, accum=None):
+        kw = {}
+        if func == F.Copy and (bias is not None or scale is not None):
+            func = F.Identity
+        if bias is not None:
+            kw["bias"] = bias
+        if scale is not None:
+            kw["scale"] = scale
+
+        def f():
+            k2 = {k: x(v) for k, v in kw.items()}
+            if accum is not None:
+                k2["accum_out"] = x(accum)
+            return g.scalar.activation(x(out), x(a), func, **k2)
+        rate = 1.6 if a[0] == "IND" else 1.0
+        return add("a", [f], [a, bias, scale], [out] + ([accum] if accum is not None else []), 0.07 + max(64, n_of(out) * rate) * CY)
+
+    def mm(items):
+        fns, rd, wr, cost = [], [], [], 0.06
+        for (o, l, r, s, e) in items:
+            fns.append(lambda o=o, l=l, r=r, s=s, e=e: g.tensor.matmul(x(o), x(l), x(r), s, e))
+            rd += [l, r]
+            wr.append(o)
+            if not s:
+                rd.append(o)
+            cost += max(64, n_of(r)) * CY * (4 if LOG[r[0]][2] == "float32" else 1)
+        return add("t", fns, list(dict.fromkeys(rd)), list(dict.fromkeys(wr)), cost)
+
+    def dma(q, out, a, extra=()):
+        s = "d%d" % dn[0]
+        dn[0] += 1
+        return add(q, [lambda: Q[q].dma_start(x(out), x(a))], [a], [out], 0.1 if q != "g" else 1.0, "d", 2.2, s, 16, extra)
+
+    def remote(tag, out, a):
+        eng = topo.engines(core, nxt)
+        m = 0
+        ne = 8
+        for e in eng[:ne]:
+            m |= 1 << e
+        rid, pid = topo.addr(nxt)[0], topo.addr(nxt)[1]
+        ra, la = T.sem["a" + tag], T.sem["l" + tag]
+        i = add("g", [lambda: g.remote_dma(ap(out), ap(a), ra, la, pid, rid, m)], [a], [], 1.2, "r", 2.5, "l" + tag, ne)
+        return add("x", [], [], [out], 0.0, "x", 0.0, "a" + tag, ne, (i,))
+
+    PS = set("p%d" % i for i in range(8))
+    ring = [[0] for _ in range(NCH)]
+
+    def bank(c):
+        i = ring[c][0]
+        ring[c][0] = (i + 1) % (NB - 1)
+        return "p%d" % (c * NB + i)
+
+    def wbank(c):
+        return "p%d" % (c * NB + NB - 1)
+
+    for j in range(4):
+        c0, c1 = j * 1024, (j + 1) * 1024
+        dma("s", R("er", c0, c1), R("eff", c0, c1))
+        dma("a", R("tq", c0, c1), R("req", c0, c1))
+    dma("a", R("sti"), R("st0"))
+    dma("s", R("barl"), R("bar"))
+    for k in range(16):
+        dma("s", R("actk", None, None, 1, (k, 128, 16)), R("act", 16 * k, 16 * k + 16))
+        dma("a", R("whyk", None, None, 1, (k, 128, 16)), R("why", 16 * k, 16 * k + 16))
+
+    def iota(out, pattern, base, cm):
+        add("g", [lambda: g.iota(x(out), pattern, base, cm)], [], [out], 0.13 + 2 * n_of(out) * CY)
+    iota(R("ip"), [[0, 128]], 0, 1)
+    iota(R("ic"), [[1, 128]], 0, 0)
+    iota(R("xbi"), [[256, NJ]], 0, 0)
+    for c in range(NCH):
+        iota(R("vb_%d" % c), [[16, NJ]], LC * c, 0)
+    ts(R("gp"), R("ip"), 4, A.arith_shift_right)
+    ts(R("gc"), R("ic"), 4, A.arith_shift_right)
+    ts(R("kp"), R("ip"), 15, A.bitwise_and)
+    ts(R("kc"), R("ic"), 15, A.bitwise_and)
+    tt(R("blk"), R("gp"), R("gc"), A.is_equal)
+    ts(R("ns"), R("blk"), -64.0, A.mult, 64.0, A.add)
+    tt(R("cc"), R("kc"), R("ns"), A.add)
+    tt(R("pp"), R("kp"), R("ns"), A.add)
+    tt(R("dd"), R("kc"), R("pp"), A.subtract)
+    ts(R("eye"), R("dd"), 0.0, A.is_equal)
+    ts(R("str"), R("dd"), 1.0, A.is_ge)
+    ts(R("tri"), R("dd"), 0.0, A.is_ge)
+    for nm, de in (("shd", 1.0), ("sh1", -1.0), ("sh2", -2.0), ("sh4", -4.0), ("sh8", -8.0)):
+        ts(R("hb0", 0, 128), R("dd"), de, A.is_equal)
+        if nm == "sh1":
+            ts(R("mag"), R("dd"), -1.0, A.is_equal)
+        tt(R(nm), R("hb0", 0, 128), R("eye"), A.subtract)
+    for nm, f in (("neg", -1.0), ("i4", 4.0), ("im85", -8.5), ("i85", 8.5), ("i512", -512.0), ("i143", 143.0), ("i18", 18.0), ("i2048", 2048.0)):
+        ts(R(nm), R("eye"), f, A.mult)
+    ts(R("mt"), R("str"), -32.0, A.mult)
+    tt(R("first"), R("mt"), R("eye"), A.add)
+    ts(R("half"), R("first"), 0.5, A.mult)
+    ts(R("mr"), R("eye"), -64.0, A.mult)
+    tt(R("mr"), R("mr"), R("str"), A.add)
+    ts(R("hb0", 0, 128), R("pp"), 0.0, A.is_equal)
+    ts(R("mt"), R("sh1"), -2.0, A.mult)
+    tt(R("mt"), R("mt"), R("hb0", 0, 128), A.subtract)
+    ts(R("thf"), R("dd"), 5.0, A.min, 8.0 * LN2, A.mult)
+    ts(R("kcol", 0, 1), R("kp", 0, 1), 1.0, A.mult)
+    add("v", [lambda: g.vector.memset(x(R("m1c", 0, 1)), 56.0 * LN2 + math.log(0.7))], [], [R("m1c", 0, 1)], 0.1)
+    add("v", [lambda: g.vector.memset(x(R("m1c", 1, 2)), 60.0 * LN2)], [], [R("m1c", 1, 2)], 0.1)
+    add("v", [lambda: g.vector.memset(x(R("m1c", 2, 3)), 40.0 * LN2 + math.log(0.7 / 24.0))], [], [R("m1c", 2, 3)], 0.1)
+    act(R("mth"), R("thf"), F.Exp, R("m1c", 0, 1))
+    ts(R("blkz"), R("blk"), 1.0 / 24.0, A.mult)
+    ts(R("nblk"), R("blk"), -1.0, A.mult)
+    for k in range(16):
+        ts(R("wk", 128 * k, 128 * k + 128), R("cc"), float(k), A.is_equal)
+        ts(R("kw", 128 * k, 128 * k + 128), R("cc"), float(k), A.is_equal, R("kcol", 0, 1), A.mult)
+        ts(R("br", 128 * k, 128 * k + 128), R("pp"), float(k), A.is_equal)
+    if MACT:
+        ts(R("wh", 128 * (16 - MACT), 2048), R("wk", 128 * (16 - MACT), 2048), 0.5, A.mult)
+    ts(R("kap", 0, 1), R("kcol", 0, 1), 241.0, A.mult, 37.0, A.add)
+    ts(R("cq", 0, 1), R("kcol", 0, 1), -16.0, A.mult, 0.5, A.add)
+    ts(R("k16", 0, 1), R("kcol", 0, 1), -1.0, A.mult, 16.0, A.add)
+    ts(R("pb", 0, 1), R("kcol", 0, 1), 15.5 - MACT, A.is_ge, 40.0 * LN2, A.mult)
+    ts(R("pb", 0, 1), R("pb", 0, 1), -40.0 * LN2, A.add)
+    add("v", [lambda: g.vector.memset(x(R("thr", 0, 1)), -1.5)], [], [R("thr", 0, 1)], 0.1)
+    add("v", [lambda: g.vector.memset(x(R("ones")), 1.0)], [], [R("ones")], 0.1)
+    add("v", [lambda: g.vector.memset(x(R("allo")), 1.0 / 16.0)], [], [R("allo")], 0.1)
+    ts(R("kcol", 2, 3), R("kcol", 0, 1), 16.0, A.mult)
+    ts(R("xbase"), R("xbi"), R("kcol", 2, 3), A.add)
+    ts(R("kcol", 4, 5), R("kcol", 0, 1), 256.0, A.mult)
+    for c in range(NCH):
+        ts(R("vb_%d" % c), R("vb_%d" % c), R("kcol", 4, 5), A.add)
+    cp(R("barb"), R("barl"))
+    b = bank(0)
+    mm([(R(b, 16 * r, 16 * r + 16), R("br", 128 * r, 128 * r + 128), R("barb"), True, True) for r in range(16)])
+    cp(R("bark"), R(b, 0, 256))
+    for c in range(NCH):
+        a0, a1 = c * LC, (c + 1) * LC
+        ts(R("w0_%d" % c, 0, LC), R("actk", a0, a1), -2048.0, A.add)
+        ts(R("w0_%d" % c, LC, 2 * LC), R("whyk", a0, a1), -2047.0, A.add)
+    ts(R("sth"), R("sti"), 8.0, A.is_ge, 144.0, A.mult)
+    tt(R("stc"), R("sti"), R("sth"), A.add)
+    for r in range(16):
+        c, o = divmod(16 * r, LC)
+        ts(R("s0_%d" % c, o, o + 16), R("stc", r, 256, 16), -20.0, A.add)
+
+    def code(dst, src, cl, hh, c, n):
+        ts(cl, src, 4.0, A.max, 11.0, A.min)
+        ts(hh, src, 12.0, A.is_ge)
+        b = bank(c)
+        mm([(R(b, 0, n), R("eye"), src, True, False), (R(b, 0, n), R("neg"), cl, False, False), (R(b, 0, n), R("i143"), hh, False, True)])
+        act(dst, R(b, 0, n), F.Copy, -8.0)
+    for j in range(8):
+        c0, c1 = 512 * j, 512 * j + 512
+        d = 512 * (j % 4)
+        code(R("gt", c0, c1), R("er", c0, c1), R("kb%d" % (j // 4), d, d + 512), R("zb%d" % (j // 4), d, d + 512), j % 2, 512)
+    for j in range(4):
+        c0, c1 = 1024 * j, 1024 * j + 1024
+        ts(R("nt", c0, c1), R("tq", c0, c1), 12.0, A.is_lt, -BIG, A.mult)
+
+    def run(t, c):
+        def K(n, *a):
+            return R("%s_%d" % (n, c), *a)
+        gb, kb, zb, fl = "gb%d" % c, "kb%d" % c, "zb%d" % c, "fl%d" % c
+        w, s = "w%d_%d" % (t, c), "s%d_%d" % (t, c)
+        ts(K("off"), R(w, 0, LC), 2048.0, A.add)
+        act(R(gb, 1, CA + 1), ind(R("gt"), K("off")), F.Copy)
+        act(K("e15"), R(gb, 16, CA + 1, 16), F.Copy, 4.0)
+        act(R(gb, 0, CA, 16), R(s), F.Copy)
+        ts(R(kb), R(gb, 0, CA), -8.0, A.is_equal)
+        add("v", [lambda: g.vector.tensor_tensor_scan(x(R(zb)), x(R(kb)), x(R(gb, 0, CA)), 0.0, A.mult, A.add)], [R(kb), R(gb, 0, CA)], [R(zb)], vc(CA, 0.5))
+        tt(R(fl), ind(R("nt"), K("off")), R(zb), A.is_gt)
+        b = bank(c)
+        mm([(R(b, 0, LC), R("wk", 128 * k, 128 * k + 128), R(fl, k, CA, 16), k == 0, k == 15) for k in range(16)])
+        act(K("ov"), R(b, 0, LC), F.Sign, R("thr", 0, 1))
+        ts(K("k15"), K("e15"), -4.0, A.is_equal)
+        tt(K("t15"), K("k15"), R(zb, 15, CA, 16), A.mult)
+        tt(K("f4"), K("t15"), K("e15"), A.add)
+        ts(K("y7"), K("f4"), 7, A.bitwise_and)
+        ts(K("h8"), K("f4"), 4.0, A.is_ge, 8.0, A.mult)
+        tt(K("val"), K("y7"), K("h8"), A.add)
+        if t < VI - 1:
+            b = bank(c)
+            mm([(R(b, 0, LC), R("eye"), K("val"), True, False), (R(b, 0, LC), R("i18"), K("h8"), False, True)])
+            act(R("so%d_%d" % (t, c)), R(b, 0, LC), F.Copy, -20.0)
+            remote("s%d_%d" % (t, c), R("s%d_%d" % (t + 1, c)), R("so%d_%d" % (t, c)))
+
+    def lists(c, mat, src, extra=()):
+        b = bank(c)
+        it = [(R(b, 0, NJ), R(mat, 128 * r, 128 * r + 128), R(src, r, LC, 16), r == 0, r == 15 and not extra) for r in range(16)]
+        for (l, r_) in extra:
+            it.append((R(b, 0, NJ), l, r_, False, True))
+        mm(it)
+        return R(b, 0, NJ)
+
+    def cand(t, c):
+        def K(n, *a):
+            return R("%s_%d" % (n, c), *a)
+        w = "w%d_%d" % (t, c)
+        S_, Q_ = R(w, 0, LC), R(w, LC, 2 * LC)
+        b = bank(c)
+        mm([(R(b, 0, LC), R("half"), K("ov"), True, True)])
+        act(K("X"), R(b, 0, LC), F.Relu, R("cq", 0, 1))
+        p = lists(c, "kw", "X_%d" % c, [(R("eye"), R("xbase"))])
+        cp(K("xl", 0, NJ), p)
+        tt(K("xs"), K("X"), S_, A.mult)
+        p = lists(c, "wk", "xs_%d" % c)
+        ts(K("sl", 0, NJ), p, 2048.0, A.add)
+        b = bank(c)
+        mm([(R(b, 0, LC), R("mth"), K("X"), True, True)])
+        act(K("tj"), R(b, 0, LC), F.Copy)
+        act(K("zx"), ind(R("zb%d" % c), K("xl", 0, NJ)), F.Copy)
+        act(K("nx"), ind(R("nt"), K("sl", 0, NJ)), F.Copy)
+        ts(K("hx"), K("zx"), 0.0, A.is_ge)
+        b = bank(c)
+        mm([(R(b, 0, LC), R("eye"), K("zx"), True, False), (R(b, 0, LC), R("i512"), K("hx"), False, False), (R(b, 0, LC), R("eye"), K("nx"), False, True)])
+        act(K("w8"), R(b, 0, LC), F.Exp, R("m1c", 1, 2), LN2)
+        ts(K("f1"), K("w8"), 0.0, A.is_gt)
+        b = bank(c)
+        mm([(R(b, 0, LC), R("blk"), K("w8"), True, True)])
+        tt(K("T"), R(b, 0, LC), K("tj"), A.is_ge)
+        b = bank(c)
+        mm([(R(b, 0, LC), R("mt"), K("T"), True, False), (R(b, 0, LC), R("eye"), K("X"), False, True)])
+        act(K("D"), R(b, 0, LC), F.Relu)
+        tt(K("ds"), K("D"), S_, A.mult)
+        b = bank(c)
+        pw = wbank(c)
+        mm([(R(b, 0, LC), R("blk"), K("xs"), True, False), (R(b, 0, LC), R("i2048"), R("ones", 0, LC), False, True),
+            (R(b, LC, 2 * LC), R("blk"), K("ds"), True, False), (R(b, LC, 2 * LC), R("i2048"), R("ones", 0, LC), False, True)])
+        mm([(R(pw, 2 * LC, 3 * LC), R("blk"), K("ds"), True, False), (R(pw, 2 * LC, 3 * LC), R("eye"), R("ones", 0, LC), False, True)])
+        act(K("sx"), R(b, 0, LC), F.Copy)
+        act(R(b, 2 * LC, 3 * LC), R(b, 0, LC), F.Copy, float(97 * t), R("kap", 0, 1))
+        tt(K("pr"), R(b, LC, 2 * LC), K("sx"), A.mult)
+        ts(K("sh"), K("pr"), 5, A.arith_shift_right)
+        tt(K("sm"), K("sh"), R(b, 2 * LC, 3 * LC), A.add)
+        ts(K("ci"), K("sm"), 4095, A.bitwise_and)
+        cp(K("c16"), K("ci"))
+        ts(K("cf"), K("ci"), -2048.0, A.add)
+        tt(K("qe"), Q_, R(pw, 2 * LC, 3 * LC), A.is_equal)
+        act(R("cg%d" % c), ind(R("gt"), K("c16")), F.Copy)
+        b = bank(c)
+        mm([(R(b, 0, LC), R("im85"), K("hx"), True, False), (R(b, 0, LC), R("eye"), K("nx"), False, True)])
+        hb, cg = "hb%d" % c, "cg%d" % c
+        for m in range(16 - MACT):
+            tt(R(hb, m * LC, (m + 1) * LC), R(cg, m, CA, 16), R(b, 0, LC), A.is_gt)
+        for m0 in range(16 - MACT, 16, 512 // LC):
+            b = bank(c)
+            k = min(512 // LC, 16 - m0)
+            it = []
+            for m in range(m0, m0 + k):
+                o = R(b, (m - m0) * LC, (m - m0 + 1) * LC)
+                it += [(o, R("eye"), R(cg, m, CA, 16), True, False), (o, R("i85"), K("hx"), False, False), (o, R("neg"), K("nx"), False, True)]
+            mm(it)
+            act(R(hb, m0 * LC, (m0 + k) * LC), R(b, 0, k * LC), F.Sign)
+        b = bank(c)
+        mm([(R(b, 0, LC), R("wk" if m < 16 - MACT else "wh", 128 * m, 128 * m + 128), R(hb, m * LC, (m + 1) * LC), m == 0, m == 15) for m in range(16)])
+        act(K("pw"), R(b, 0, LC), F.Exp, R("pb", 0, 1), 5.0 * LN2)
+        b = bank(c)
+        mm([(R(b, 0, LC), R("nblk"), K("f1"), True, False), (R(b, 0, LC), R("eye"), R("bark", c * LC, (c + 1) * LC), False, True)])
+        act(K("tb"), R(b, 0, LC), F.Exp, R("m1c", 2, 3), 5.0 * LN2)
+        b = bank(c)
+        mm([(R(b, 0, LC), R("blkz"), K("pw"), True, True)])
+        tt(K("eq"), R(b, 0, LC), K("pw"), A.is_le)
+        tt(K("insi"), R(b, 0, LC), K("tb"), A.is_ge)
+        b = bank(c)
+        mm([(R(b, 0, LC), R("first"), K("eq"), True, True),
+            (R(b, LC, 2 * LC), R("blk"), K("X"), True, False), (R(b, LC, 2 * LC), R("neg"), K("insi"), False, True),
+            (R(b, 2 * LC, 3 * LC), R("tri"), K("X"), True, False), (R(b, 2 * LC, 3 * LC), R("eye"), K("insi"), False, True),
+            (R(b, 3 * LC, 4 * LC), R("eye"), K("X"), True, False), (R(b, 3 * LC, 4 * LC), R("eye"), K("insi"), False, True)])
+        act(K("ret"), R(b, LC, 2 * LC), F.Relu, accum=R("ac%d_%d" % (t, c), 0, 1))
+        act(K("M"), R(b, 0, LC), F.Relu)
+        ts(K("mi"), R(b, 2 * LC, 3 * LC), -1.0, A.add, 0.0, A.max)
+        ts(K("xi"), R(b, 3 * LC, 4 * LC), -1.0, A.add, 0.0, A.max)
+        tt(K("mc"), K("M"), K("cf"), A.mult)
+        mm([(R(pw, 3 * LC, 4 * LC), R("blk"), K("mc"), True, True)])
+        tt(K("iv", 0, LC), K("xi"), R(pw, 3 * LC, 4 * LC), A.mult)
+        tt(K("iv", LC, 2 * LC), K("xi"), R(pw, 2 * LC, 3 * LC), A.mult)
+        b = bank(c)
+        mm([(R(b, 0, LC), R("eye"), K("D"), True, False), (R(b, 0, LC), R("eye"), K("qe"), False, False), (R(b, 0, LC), R("i4"), K("ret"), False, True)])
+        ts(K("go"), R(b, 0, LC), 4.5, A.is_ge)
+        b = bank(c)
+        mm([(R(b, 0, LC), R("blk"), K("go"), True, True), (R(b, LC, 2 * LC), R("mr"), K("go"), True, True)])
+        act(K("rb"), R(b, LC, 2 * LC), F.Relu)
+        ts(K("fm"), R(b, 0, LC), R("k16", 0, 1), A.is_ge)
+        pr = R(b, LC, 2 * LC)
+        wp = R(pw, 0, 2 * LC)
+        wS, wQ = R(pw, 0, LC), R(pw, LC, 2 * LC)
+        mm([(wp, R("eye"), R(w, 0, 2 * LC), True, True)])
+
+        def prod(n, mask):
+            tt(K(n, 0, LC), wS, mask, A.mult)
+            tt(K(n, LC, 2 * LC), wQ, mask, A.mult)
+        prod("a1", K("mi"))
+        prod("a2", K("go"))
+        tt(K("fi", 0, LC), K("fm"), K("cf"), A.mult)
+        ts(K("fi", LC, 2 * LC), K("fm"), -2048.0, A.mult)
+        base, moves = R(w, 0, 2 * LC), [("shd", "a1"), ("neg", "a2")]
+        for s in range(4):
+            ts(K("ri"), pr, 0.0, A.max)
+            ts(K("mk"), K("ri"), s, A.arith_shift_right, 1, A.bitwise_and)
+            prod("m%d" % s, K("mk"))
+            moves.append(("sh%d" % (1 << s), "m%d" % s))
+            if s < 3:
+                tt(K("ar"), pr, K("mk"), A.mult)
+                b = bank(c)
+                pr2 = R(b, 0, LC)
+                mm([(pr2, R("eye"), K("rb"), True, False), (pr2, R("sh%d" % (1 << s)), K("ar"), False, True)])
+                pr = pr2
+                if s < 2:
+                    act(K("rb"), pr, F.Copy)
+            if s == 3:
+                moves += [("eye", "iv"), ("eye", "fi")]
+            mm([(wp, R("eye"), base, True, False)] + [(wp, R(m), K(a), False, q == len(moves) - 1) for q, (m, a) in enumerate(moves)])
+            if s == 1:
+                cp(K("wb"), wp)
+                base, moves = K("wb"), []
+        if t < VI - 1:
+            wo = "wo%d_%d" % (t, c)
+            cp(R(wo), wp)
+            remote("p%d_%d" % (t, c), R("w%d_%d" % (t + 1, c)), R(wo))
+        else:
+            act(R("ysk", c * LC, (c + 1) * LC), wS, F.Copy, 2048.0)
+            act(R("ywk", c * LC, (c + 1) * LC), wQ, F.Copy, 2047.0)
+
+    def table(t, c):
+        def K(n, *a):
+            return R("%s_%d" % (n, c), *a)
+        p = lists(c, "wk", "val_%d" % c)
+        cp(K("ui"), p)
+        ts(K("uj"), K("ui"), 15, A.bitwise_and)
+        tt(K("uk"), K("uj"), K("vb"), A.add)
+        cp(K("vl", 0, NJ), K("uk"))
+        act(K("eo"), ind(R("er"), K("vl", 0, NJ)), F.Copy)
+        tt(K("es"), K("eo"), K("val"), A.add)
+        ts(K("eh"), K("es"), 1, A.arith_shift_right)
+        cp(K("ne"), K("eh"))
+        if t < VI - 1:
+            code(K("ng"), K("ne"), K("cl"), K("hh"), c, LC)
+        cp(ind(R("er"), K("vl", 0, NJ)), K("ne"))
+        if t < VI - 1:
+            cp(ind(R("gt"), K("vl", 0, NJ)), K("ng"))
+
+    def count(t):
+        b = bank(0)
+        mm([(R(b, 0, 1), R("allo"), R("ac%d_%d" % (t, c), 0, 1), c == 0, c == NCH - 1) for c in range(NCH)])
+        cp(R("rci", 0, 1), R(b, 0, 1))
+        ts(R("rci", 4, 5), R("rci", 0, 1), 1, A.bitwise_and)
+        ts(R("thr", 0, 1), R("rci", 4, 5), -1.0, A.mult, -1.5, A.add)
+
+    for t in range(VI):
+        for c in range(NCH):
+            run(t, c)
+        for c in range(NCH):
+            cand(t, c)
+        for c in range(NCH):
+            table(t, c)
+        if t < VI - 1:
+            count(t)
+    for j in range(2):
+        dma("s" if j else "a", R("ye", 2048 * j, 2048 * j + 2048), R("er", 2048 * j, 2048 * j + 2048))
+    for k in range(16):
+        dma("s", R("ys", 16 * k, 16 * k + 16), R("ysk", None, None, 1, (k, 128, 16)))
+        dma("a", R("yw", 16 * k, 16 * k + 16), R("ywk", None, None, 1, (k, 128, 16)))
+
+    n = len(ops)
+    HOP = 0.12
+    tail = [0.0] * n
+    succ = [[] for _ in range(n)]
+    for i, o in enumerate(ops):
+        for d in o["deps"]:
+            succ[d].append(i)
+    for i in range(n - 1, -1, -1):
+        o = ops[i]
+        m = 0.0
+        for j in succ[i]:
+            m = max(m, tail[j])
+        tail[i] = m + o["cost"] + o["lat"] + HOP
+    ndep = [len(o["deps"]) for o in ops]
+    ready = [0.0] * n
+    avail = [i for i in range(n) if ndep[i] == 0]
+    free = {q: 0.0 for q in "vatgsx"}
+    order = []
+    while avail:
+        best = None
+        for i in avail:
+            q = ops[i]["q"]
+            st = ready[i] if q == "x" else max(ready[i], free[q])
+            key = (round(st, 2), -tail[i], i)
+            if best is None or key < best[0]:
+                best = (key, i, st)
+        _, i, st = best
+        avail.remove(i)
+        o = ops[i]
+        if o["q"] != "x":
+            free[o["q"]] = st + o["cost"]
+        fin = st + o["cost"] + o["lat"]
+        order.append(i)
+        for j in succ[i]:
+            ready[j] = max(ready[j], fin + (HOP if ops[j]["q"] != o["q"] else 0.03))
+            ndep[j] -= 1
+            if ndep[j] == 0:
+                avail.append(j)
+
+    cnt = {"qv": 0, "qa": 0, "qt": 0, "qg": 0}
+    known = {q: {} for q in "vatgs"}
+    done = {}
+    tot = {}
+
+    def wait(q, sem, v):
+        if known[q].get(sem, 0) < v:
+            Q[q].wait_ge(T.sem[sem], v)
+            known[q][sem] = v
+
+    for i in order:
+        o = ops[i]
+        q = o["q"]
+        if q == "x":
+            done[i] = (o["sem"], o["inc"], {o["sem"]: o["inc"]})
+            tot[o["sem"]] = o["inc"]
+            continue
+        for d in sorted(o["deps"], key=lambda d: -order.index(d) if False else d, reverse=True):
+            sem, v, clk = done[d]
+            if known[q].get(sem, 0) < v:
+                wait(q, sem, v)
+                for s2, v2 in clk.items():
+                    if known[q].get(s2, 0) < v2:
+                        known[q][s2] = v2
+        for f in o["fns"]:
+            r = f()
+            if o["kind"] == "c":
+                s = QS[q]
+                cnt[s] += 1
+                r.then_inc(T.sem[s], 1)
+            elif o["kind"] == "d":
+                r.then_inc(T.sem[o["sem"]], 16)
+        clk = dict(known[q])
+        if o["kind"] == "c":
+            s = QS[q]
+            clk[s] = cnt[s]
+            done[i] = (s, cnt[s], clk)
+            tot[s] = cnt[s]
+        else:
+            clk[o["sem"]] = o["inc"]
+            done[i] = (o["sem"], o["inc"], clk)
+            tot[o["sem"]] = o["inc"]
+    for s, v in tot.items():
+        wait("g", s, v)

@@ -7,18 +7,19 @@ NCH, W, L, VI = 2, 4096, 16, 4
 LC = 256 // NCH
 CA = LC * L
 NJ = LC // 16
-MACT = 4
+NP = 2
 LN2 = math.log(2.0)
 BIG = 1024.0
 NDMA = 80
+NB = 8 // NCH
+BIAS = {"run0": 2.8, "end0": -2.9, "head0": 8.4, "net0": 6.9, "score0": 7.1, "fin0": 10.8, "fin1": -3.5, "run1": -9.1,
+        "net1": -3.7, "head1": 2.9, "score1": -2.5, "end1": -2.0, "tab": -10.2}
 
 SCRATCH = {}
 SEMAPHORES = ["qv", "qa", "qt", "qg"] + ["d%d" % i for i in range(NDMA)]
 for _t in range(VI - 1):
     for _c in range(NCH):
         SEMAPHORES += ["ap%d_%d" % (_t, _c), "as%d_%d" % (_t, _c), "lp%d_%d" % (_t, _c), "ls%d_%d" % (_t, _c)]
-
-
 LOG = {}
 _SHORT = {"bfloat16": "bf", "float16": "hf", "float32": "ff", "int32": "nn", "uint16": "uu"}
 
@@ -39,55 +40,52 @@ for _n in ("er", "gt", "nt", "tq"):
 for _n in ("ip", "ic", "gp", "gc", "kp", "kc"):
     _buf(_n, 128, "int32")
 for _n in ("dd", "cc", "pp", "ns", "eye", "blk", "str", "tri", "first", "half", "shd", "sh1", "sh2", "sh4", "sh8", "neg",
-           "i4", "im85", "i85", "i512", "i143", "i18", "i2048", "mt", "mth", "mr", "blkz", "mag", "ones", "nblk"):
+           "i4", "im85", "i512", "i71", "i72", "i2048", "mt", "mth", "mr", "blkz", "ones", "nblk", "blk4"):
     _buf(_n, 128, "bfloat16")
-for _n in ("wk", "kw", "br", "wh"):
+for _n in ("wk", "br"):
     _buf(_n, 16 * 128, "bfloat16")
 _buf("thf", 128, "float32")
 _buf("allo", 128, "float32")
-for _n in ("kcol", "kap", "cq", "k16", "pb", "thr", "m1c"):
+for _n in ("kcol", "kap", "cq", "k16", "thr", "m1c"):
     _buf(_n, 8, "float32")
 _buf("rci", 8, "int32")
-_buf("xbase", NJ, "bfloat16")
+_buf("xbase", 2 * NJ, "bfloat16")
 _buf("xbi", NJ, "int32")
 _buf("barl", 16, "int32")
 _buf("barb", 16, "bfloat16")
-_buf("bark", 256, "bfloat16")
+for _n in ("bark", "sti", "sth", "stc"):
+    _buf(_n, 256, "bfloat16")
 _buf("actk", 256, "int32")
 _buf("whyk", 256, "int32")
-_buf("sti", 256, "bfloat16")
-_buf("sth", 256, "bfloat16")
-_buf("stc", 256, "bfloat16")
 _buf("ysk", 256, "float32")
 _buf("ywk", 256, "float32")
 for _c in range(NCH):
     for _t in range(VI):
-        _buf("w%d_%d" % (_t, _c), 256 * LC // 128, "float16")
-        _buf("wo%d_%d" % (_t, _c), 256 * LC // 128, "float16")
+        _buf("w%d_%d" % (_t, _c), 2 * LC, "float16")
+        _buf("wo%d_%d" % (_t, _c), 2 * LC, "float16")
         _buf("s%d_%d" % (_t, _c), LC, "bfloat16")
         _buf("so%d_%d" % (_t, _c), LC, "bfloat16")
         _buf("ac%d_%d" % (_t, _c), 8, "float32")
     _buf("gb%d" % _c, CA + 16, "bfloat16")
     for _n in ("kb", "zb", "fl", "cg", "hb"):
         _buf("%s%d" % (_n, _c), CA, "bfloat16")
-    for _n in ("e15", "k15", "t15", "val", "h8", "ov", "X", "zx", "nx", "hx", "w8", "f1", "T", "D", "pw", "eq", "M", "insi",
-               "mi", "xi", "ret", "qe", "go", "fm", "rb", "ar", "eo", "ne", "cl", "hh", "ng"):
+    for _n in ("e15", "k15", "t15", "val", "h8", "ov", "X", "zx", "nx", "hx", "w8", "f1", "T", "D", "pw", "pv", "eq", "M",
+               "insi", "nin", "mi", "xi", "ret", "qe", "go", "fm", "rb", "ar", "eo", "ne", "cl", "hh", "ng"):
         _buf("%s_%d" % (_n, _c), LC, "bfloat16")
-    for _n in ("xs", "ds", "cf", "mc"):
+    for _n in ("ds", "cf", "mc"):
         _buf("%s_%d" % (_n, _c), LC, "float16")
-    for _n in ("a1", "a2", "m0", "m1", "m2", "m3", "wb", "iv", "fi"):
+    for _n in ("a1", "a2", "m0", "m1", "m2", "m3", "wb", "iv", "fi", "xq"):
         _buf("%s_%d" % (_n, _c), 2 * LC, "float16")
-    for _n in ("f4", "y7", "pr", "sh", "sm", "ci", "ri", "mk", "es", "eh"):
+    for _n in ("f4", "y7", "pr", "sh", "sm", "ci", "ri", "mk", "eh"):
         _buf("%s_%d" % (_n, _c), LC, "int32")
     for _n in ("tj", "sx", "tb"):
         _buf("%s_%d" % (_n, _c), LC, "float32")
     for _n in ("off", "c16"):
         _buf("%s_%d" % (_n, _c), LC, "uint16")
-    for _n in ("xl", "sl", "vl"):
-        _buf("%s_%d" % (_n, _c), max(NJ, 2), "uint16")
+    _buf("xl_%d" % _c, 2 * NJ, "uint16")
+    _buf("vl_%d" % _c, NJ, "uint16")
     for _n in ("ui", "uj", "uk", "vb"):
         _buf("%s_%d" % (_n, _c), NJ, "int32")
-NB = 8 // NCH
 for _i in range(8):
     _buf("p%d" % _i, 512, "float32", "psum")
 
@@ -112,6 +110,8 @@ def rank_program(g, core, T, topo):
     Q = {"v": g.vector, "a": g.scalar, "t": g.tensor, "g": g, "s": g.sync}
     QS = {"v": "qv", "a": "qa", "t": "qt", "g": "qg"}
     dn = [0]
+    PH = ["set"]
+    PS = set("p%d" % i for i in range(8))
 
     def R(name, a=None, b=None, st=1, p=None):
         n = LOG[name][1] if name in LOG else T[name].shape[1]
@@ -156,8 +156,6 @@ def rank_program(g, core, T, topo):
             for r in lst:
                 ps = r[0] in PS
                 for (j, r2, w2) in acc.get(r[0], ()):
-                    if j == i:
-                        continue
                     if ps and ops[j]["q"] != q:
                         deps.add(j)
                     elif (isw or w2) and overlap(r, r2):
@@ -165,26 +163,22 @@ def rank_program(g, core, T, topo):
         for lst, isw in ((rd, False), (wr, True)):
             for r in lst:
                 cur = acc.setdefault(r[0], [])
-                ps = r[0] in PS
-                if isw and r[3] == 1 and r[4] is None and not ps:
+                if isw and r[3] == 1 and r[4] is None and r[0] not in PS:
                     cur[:] = [e for e in cur if not (e[1][1] >= r[1] and e[1][2] <= r[2])]
                 cur.append((i, r, isw))
-                if ps and isw:
-                    cur[:] = [e for e in cur if e[0] >= i - 1500]
-        ops.append({"q": q, "fns": fns, "deps": deps, "cost": cost, "kind": kind, "lat": lat, "sem": sem, "inc": inc})
+        ops.append({"ph": PH[0], "q": q, "fns": fns, "deps": deps, "cost": cost, "kind": kind, "lat": lat, "sem": sem, "inc": inc})
         return i
 
     def two(*rs):
         return all(isinstance(r, tuple) and r[0] in LOG and LOG[r[0]][2] in ("bfloat16", "float16", "uint16") and r[0] not in PS for r in rs)
 
-    CY = 0.00105
+    CY = 0.00083
 
     def vc(n, rate):
-        return 0.05 + max(64, n * rate) * CY
+        return 0.02 + max(64, n * rate) * CY
 
     def tt(out, a, b, op):
-        i = a[0] == "IND"
-        rate = 1.6 if i or out[0] == "IND" else (1.0 if (a[0][0] == "p" and a[0] in PS) or (b[0] in PS) else 2.0)
+        rate = 1.6 if a[0] == "IND" else (1.0 if a[0] in PS or b[0] in PS else 2.0)
         return add("v", [lambda: g.vector.tensor_tensor(x(out), x(a), x(b), op)], [a, b], [out], vc(n_of(out), rate))
 
     def ts(out, a, s1, op0, s2=None, op1=None):
@@ -196,9 +190,14 @@ def rank_program(g, core, T, topo):
         return add("v", [f], [a, s1, s2], [out], vc(n_of(out), rate))
 
     def cp(out, a):
-        sc = out[0] == "IND"
-        rate = 4.0 if sc else (0.5 if two(out, a) else 1.0)
+        rate = 4.0 if out[0] == "IND" else (0.5 if two(out, a) else 1.0)
         return add("v", [lambda: g.vector.tensor_copy(x(out), x(a))], [a], [out], vc(n_of(a), rate))
+
+    def fill(out, v):
+        add("v", [lambda: g.vector.memset(x(out), v)], [], [out], 0.1)
+
+    def scan(out, d0, d1):
+        add("v", [lambda: g.vector.tensor_tensor_scan(x(out), x(d0), x(d1), 0.0, A.mult, A.add)], [d0, d1], [out], vc(n_of(out), 0.5))
 
     def act(out, a, func, bias=None, scale=None, accum=None):
         kw = {}
@@ -208,49 +207,44 @@ def rank_program(g, core, T, topo):
             kw["bias"] = bias
         if scale is not None:
             kw["scale"] = scale
-
-        def f():
-            k2 = {k: x(v) for k, v in kw.items()}
-            if accum is not None:
-                k2["accum_out"] = x(accum)
-            return g.scalar.activation(x(out), x(a), func, **k2)
+        if accum is not None:
+            kw["accum_out"] = accum
         rate = 1.6 if a[0] == "IND" else 1.0
-        return add("a", [f], [a, bias, scale], [out] + ([accum] if accum is not None else []), 0.07 + max(64, n_of(out) * rate) * CY)
+        return add("a", [lambda: g.scalar.activation(x(out), x(a), func, **{k: x(v) for k, v in kw.items()})], [a, bias, scale],
+                   [out] + ([accum] if accum is not None else []), 0.04 + max(64, n_of(out) * rate) * CY)
 
     def mm(items):
-        fns, rd, wr, cost = [], [], [], 0.06
+        fns, rd, wr, cost = [], [], [], 0.02
         for (o, l, r, s, e) in items:
             fns.append(lambda o=o, l=l, r=r, s=s, e=e: g.tensor.matmul(x(o), x(l), x(r), s, e))
             rd += [l, r]
             wr.append(o)
-            if not s:
-                rd.append(o)
             cost += max(64, n_of(r)) * CY * (4 if LOG[r[0]][2] == "float32" else 1)
         return add("t", fns, list(dict.fromkeys(rd)), list(dict.fromkeys(wr)), cost)
 
-    def dma(q, out, a, extra=()):
+    def dma(q, out, a):
         s = "d%d" % dn[0]
         dn[0] += 1
-        return add(q, [lambda: Q[q].dma_start(x(out), x(a))], [a], [out], 0.1 if q != "g" else 1.0, "d", 2.2, s, 16, extra)
+        return add(q, [lambda: Q[q].dma_start(x(out), x(a))], [a], [out], 0.1, "d", 2.2, s, 16)
 
     def remote(tag, out, a):
-        eng = topo.engines(core, nxt)
-        m = 0
-        ne = 8
-        for e in eng[:ne]:
+        m, ne = 0, 8
+        for e in topo.engines(core, nxt)[:ne]:
             m |= 1 << e
         rid, pid = topo.addr(nxt)[0], topo.addr(nxt)[1]
         ra, la = T.sem["a" + tag], T.sem["l" + tag]
         i = add("g", [lambda: g.remote_dma(ap(out), ap(a), ra, la, pid, rid, m)], [a], [], 1.2, "r", 2.5, "l" + tag, ne)
         return add("x", [], [], [out], 0.0, "x", 0.0, "a" + tag, ne, (i,))
 
-    PS = set("p%d" % i for i in range(8))
     ring = [[0] for _ in range(NCH)]
 
     def bank(c):
         i = ring[c][0]
-        ring[c][0] = (i + 1) % (NB - 1)
+        ring[c][0] = (i + 1) % (NB - 2)
         return "p%d" % (c * NB + i)
+
+    def nbank(c):
+        return "p%d" % (c * NB + NB - 2)
 
     def wbank(c):
         return "p%d" % (c * NB + NB - 1)
@@ -286,11 +280,9 @@ def rank_program(g, core, T, topo):
     ts(R("tri"), R("dd"), 0.0, A.is_ge)
     for nm, de in (("shd", 1.0), ("sh1", -1.0), ("sh2", -2.0), ("sh4", -4.0), ("sh8", -8.0)):
         ts(R("hb0", 0, 128), R("dd"), de, A.is_equal)
-        if nm == "sh1":
-            ts(R("mag"), R("dd"), -1.0, A.is_equal)
         tt(R(nm), R("hb0", 0, 128), R("eye"), A.subtract)
-    for nm, f in (("neg", -1.0), ("i4", 4.0), ("im85", -8.5), ("i85", 8.5), ("i512", -512.0), ("i143", 143.0), ("i18", 18.0), ("i2048", 2048.0)):
-        ts(R(nm), R("eye"), f, A.mult)
+    for nm, f in (("neg", -1.0), ("i4", 4.0), ("im85", -8.5), ("i512", -512.0), ("i71", 71.5), ("i72", 72.0), ("i2048", 2048.0)):
+        act(R(nm), R("eye"), F.Copy, None, f)
     ts(R("mt"), R("str"), -32.0, A.mult)
     tt(R("first"), R("mt"), R("eye"), A.add)
     ts(R("half"), R("first"), 0.5, A.mult)
@@ -301,28 +293,27 @@ def rank_program(g, core, T, topo):
     tt(R("mt"), R("mt"), R("hb0", 0, 128), A.subtract)
     ts(R("thf"), R("dd"), 5.0, A.min, 8.0 * LN2, A.mult)
     ts(R("kcol", 0, 1), R("kp", 0, 1), 1.0, A.mult)
-    add("v", [lambda: g.vector.memset(x(R("m1c", 0, 1)), 56.0 * LN2 + math.log(0.7))], [], [R("m1c", 0, 1)], 0.1)
-    add("v", [lambda: g.vector.memset(x(R("m1c", 1, 2)), 60.0 * LN2)], [], [R("m1c", 1, 2)], 0.1)
-    add("v", [lambda: g.vector.memset(x(R("m1c", 2, 3)), 40.0 * LN2 + math.log(0.7 / 24.0))], [], [R("m1c", 2, 3)], 0.1)
-    act(R("mth"), R("thf"), F.Exp, R("m1c", 0, 1))
+    BC = {}
+    for q, (nm, v) in enumerate((("thj", 56.0 * LN2 + math.log(0.7)), ("w8", 60.0 * LN2), ("tb", 40.0 * LN2 + math.log(0.7 / 24.0)),
+                                 ("f4", -3.5), ("one", -1.0), ("hi", -11.5), ("pv", -40.0 * LN2))):
+        BC[nm] = R("m1c", q, q + 1)
+        fill(BC[nm], v)
+    act(R("mth"), R("thf"), F.Exp, BC["thj"])
     ts(R("blkz"), R("blk"), 1.0 / 24.0, A.mult)
+    ts(R("blk4"), R("blk"), 4.0, A.mult)
     ts(R("nblk"), R("blk"), -1.0, A.mult)
     for k in range(16):
         ts(R("wk", 128 * k, 128 * k + 128), R("cc"), float(k), A.is_equal)
-        ts(R("kw", 128 * k, 128 * k + 128), R("cc"), float(k), A.is_equal, R("kcol", 0, 1), A.mult)
         ts(R("br", 128 * k, 128 * k + 128), R("pp"), float(k), A.is_equal)
-    if MACT:
-        ts(R("wh", 128 * (16 - MACT), 2048), R("wk", 128 * (16 - MACT), 2048), 0.5, A.mult)
     ts(R("kap", 0, 1), R("kcol", 0, 1), 241.0, A.mult, 37.0, A.add)
     ts(R("cq", 0, 1), R("kcol", 0, 1), -16.0, A.mult, 0.5, A.add)
     ts(R("k16", 0, 1), R("kcol", 0, 1), -1.0, A.mult, 16.0, A.add)
-    ts(R("pb", 0, 1), R("kcol", 0, 1), 15.5 - MACT, A.is_ge, 40.0 * LN2, A.mult)
-    ts(R("pb", 0, 1), R("pb", 0, 1), -40.0 * LN2, A.add)
-    add("v", [lambda: g.vector.memset(x(R("thr", 0, 1)), -1.5)], [], [R("thr", 0, 1)], 0.1)
-    add("v", [lambda: g.vector.memset(x(R("ones")), 1.0)], [], [R("ones")], 0.1)
-    add("v", [lambda: g.vector.memset(x(R("allo")), 1.0 / 16.0)], [], [R("allo")], 0.1)
+    fill(R("thr", 0, 1), -1.5)
+    fill(R("ones"), 1.0)
+    fill(R("allo"), 1.0 / 16.0)
     ts(R("kcol", 2, 3), R("kcol", 0, 1), 16.0, A.mult)
-    ts(R("xbase"), R("xbi"), R("kcol", 2, 3), A.add)
+    ts(R("xbase", 0, NJ), R("xbi"), R("kcol", 2, 3), A.add)
+    fill(R("xbase", NJ, 2 * NJ), 2048.0)
     ts(R("kcol", 4, 5), R("kcol", 0, 1), 256.0, A.mult)
     for c in range(NCH):
         ts(R("vb_%d" % c), R("vb_%d" % c), R("kcol", 4, 5), A.add)
@@ -340,16 +331,15 @@ def rank_program(g, core, T, topo):
         c, o = divmod(16 * r, LC)
         ts(R("s0_%d" % c, o, o + 16), R("stc", r, 256, 16), -20.0, A.add)
 
-    def code(dst, src, cl, hh, c, n):
+    def code(dst, src, cl, hh, b, n):
         ts(cl, src, 4.0, A.max, 11.0, A.min)
-        ts(hh, src, 12.0, A.is_ge)
-        b = bank(c)
-        mm([(R(b, 0, n), R("eye"), src, True, False), (R(b, 0, n), R("neg"), cl, False, False), (R(b, 0, n), R("i143"), hh, False, True)])
-        act(dst, R(b, 0, n), F.Copy, -8.0)
+        act(hh, src, F.Sign, BC["hi"])
+        mm([(R(b, 0, n), R("eye"), src, True, False), (R(b, 0, n), R("neg"), cl, False, False), (R(b, 0, n), R("i71"), hh, False, True)])
+        act(dst, R(b, 0, n), F.Copy, 63.5)
     for j in range(8):
         c0, c1 = 512 * j, 512 * j + 512
         d = 512 * (j % 4)
-        code(R("gt", c0, c1), R("er", c0, c1), R("kb%d" % (j // 4), d, d + 512), R("zb%d" % (j // 4), d, d + 512), j % 2, 512)
+        code(R("gt", c0, c1), R("er", c0, c1), R("kb%d" % (j // 4), d, d + 512), R("zb%d" % (j // 4), d, d + 512), bank(j % 2), 512)
     for j in range(4):
         c0, c1 = 1024 * j, 1024 * j + 1024
         ts(R("nt", c0, c1), R("tq", c0, c1), 12.0, A.is_lt, -BIG, A.mult)
@@ -357,60 +347,83 @@ def rank_program(g, core, T, topo):
     def run(t, c):
         def K(n, *a):
             return R("%s_%d" % (n, c), *a)
+        PH[0] = "run%d" % c
         gb, kb, zb, fl = "gb%d" % c, "kb%d" % c, "zb%d" % c, "fl%d" % c
         w, s = "w%d_%d" % (t, c), "s%d_%d" % (t, c)
         ts(K("off"), R(w, 0, LC), 2048.0, A.add)
-        act(R(gb, 1, CA + 1), ind(R("gt"), K("off")), F.Copy)
-        act(K("e15"), R(gb, 16, CA + 1, 16), F.Copy, 4.0)
-        act(R(gb, 0, CA, 16), R(s), F.Copy)
-        ts(R(kb), R(gb, 0, CA), -8.0, A.is_equal)
-        add("v", [lambda: g.vector.tensor_tensor_scan(x(R(zb)), x(R(kb)), x(R(gb, 0, CA)), 0.0, A.mult, A.add)], [R(kb), R(gb, 0, CA)], [R(zb)], vc(CA, 0.5))
-        tt(R(fl), ind(R("nt"), K("off")), R(zb), A.is_gt)
         b = bank(c)
-        mm([(R(b, 0, LC), R("wk", 128 * k, 128 * k + 128), R(fl, k, CA, 16), k == 0, k == 15) for k in range(16)])
+        for p in range(NP):
+            l0, l1 = p * LC // NP, (p + 1) * LC // NP
+            e0, e1 = 16 * l0, 16 * l1
+            act(R(gb, e0 + 1, e1 + 1), ind(R("gt"), K("off", l0, l1)), F.Copy)
+            act(K("e15", l0, l1), R(gb, e0 + 16, e1 + 1, 16), F.Copy, 4.0)
+            act(R(gb, e0, e1, 16), R(s, l0, l1), F.Copy)
+            ts(R(kb, e0, e1), R(gb, e0, e1), -8.0, A.is_equal)
+            scan(R(zb, e0, e1), R(kb, e0, e1), R(gb, e0, e1))
+            tt(R(fl, e0, e1), ind(R("nt"), K("off", l0, l1)), R(zb, e0, e1), A.is_gt)
+            mm([(R(b, l0, l1), R("wk", 128 * k, 128 * k + 128), R(fl, e0 + k, e1, 16), k == 0, k == 15) for k in range(16)])
         act(K("ov"), R(b, 0, LC), F.Sign, R("thr", 0, 1))
+        PH[0] = "end%d" % c
+        nb = nbank(c)
+        o = R(nb, 0, LC)
         ts(K("k15"), K("e15"), -4.0, A.is_equal)
         tt(K("t15"), K("k15"), R(zb, 15, CA, 16), A.mult)
-        tt(K("f4"), K("t15"), K("e15"), A.add)
+        mm([(o, R("eye"), K("t15"), True, False), (o, R("eye"), K("e15"), False, True)])
+        cp(K("f4"), o)
+        act(K("h8"), o, F.Sign, BC["f4"])
         ts(K("y7"), K("f4"), 7, A.bitwise_and)
-        ts(K("h8"), K("f4"), 4.0, A.is_ge, 8.0, A.mult)
-        tt(K("val"), K("y7"), K("h8"), A.add)
+        mm([(o, R("i4"), K("h8"), True, False), (o, R("i4"), R("ones", 0, LC), False, True)])
+        tt(K("val"), K("y7"), o, A.add)
         if t < VI - 1:
-            b = bank(c)
-            mm([(R(b, 0, LC), R("eye"), K("val"), True, False), (R(b, 0, LC), R("i18"), K("h8"), False, True)])
-            act(R("so%d_%d" % (t, c)), R(b, 0, LC), F.Copy, -20.0)
+            mm([(o, R("eye"), K("val"), True, False), (o, R("i72"), K("h8"), False, True)])
+            act(R("so%d_%d" % (t, c)), o, F.Copy, 52.0)
             remote("s%d_%d" % (t, c), R("s%d_%d" % (t + 1, c)), R("so%d_%d" % (t, c)))
+        o = R(nb, 0, NJ)
+        mm([(o, R("wk", 128 * r, 128 * r + 128), R("val_%d" % c, r, LC, 16), r == 0, r == 15) for r in range(16)])
+        cp(K("ui"), o)
+        ts(K("uj"), K("ui"), 15, A.bitwise_and)
+        tt(K("uk"), K("uj"), K("vb"), A.add)
+        cp(K("vl"), K("uk"))
+        act(K("eo"), ind(R("er"), K("vl")), F.Copy)
+        o = R(nb, 0, LC)
+        mm([(o, R("eye"), K("eo"), True, False), (o, R("eye"), K("val"), False, True)])
+        ts(K("eh"), o, 0.5, A.mult, -0.25, A.add)
+        cp(K("ne"), K("eh"))
+        if t < VI - 1:
+            code(K("ng"), K("ne"), K("cl"), K("hh"), nb, LC)
+        cp(ind(R("er"), K("vl")), K("ne"))
 
-    def lists(c, mat, src, extra=()):
-        b = bank(c)
-        it = [(R(b, 0, NJ), R(mat, 128 * r, 128 * r + 128), R(src, r, LC, 16), r == 0, r == 15 and not extra) for r in range(16)]
-        for (l, r_) in extra:
-            it.append((R(b, 0, NJ), l, r_, False, True))
-        mm(it)
-        return R(b, 0, NJ)
+    def table(t, c):
+        PH[0] = "tab"
+        if t < VI - 1:
+            cp(ind(R("gt"), R("vl_%d" % c)), R("ng_%d" % c))
 
     def cand(t, c):
         def K(n, *a):
             return R("%s_%d" % (n, c), *a)
+        PH[0] = "head%d" % c
         w = "w%d_%d" % (t, c)
         S_, Q_ = R(w, 0, LC), R(w, LC, 2 * LC)
+        pw, nb = wbank(c), nbank(c)
+        wp, n2 = R(pw, 0, 2 * LC), R(nb, 0, 2 * LC)
         b = bank(c)
         mm([(R(b, 0, LC), R("half"), K("ov"), True, True)])
         act(K("X"), R(b, 0, LC), F.Relu, R("cq", 0, 1))
-        p = lists(c, "kw", "X_%d" % c, [(R("eye"), R("xbase"))])
-        cp(K("xl", 0, NJ), p)
-        tt(K("xs"), K("X"), S_, A.mult)
-        p = lists(c, "wk", "xs_%d" % c)
-        ts(K("sl", 0, NJ), p, 2048.0, A.add)
+        ts(K("xq", 0, LC), K("X"), R("kcol", 0, 1), A.mult)
+        tt(K("xq", LC, 2 * LC), K("X"), S_, A.mult)
+        b = bank(c)
+        mm([(R(b, 0, 2 * NJ), R("wk", 128 * r, 128 * r + 128), R("xq_%d" % c, r, 2 * LC, 16), r == 0, False) for r in range(16)]
+           + [(R(b, 0, 2 * NJ), R("eye"), R("xbase"), False, True)])
+        cp(K("xl"), R(b, 0, 2 * NJ))
         b = bank(c)
         mm([(R(b, 0, LC), R("mth"), K("X"), True, True)])
         act(K("tj"), R(b, 0, LC), F.Copy)
         act(K("zx"), ind(R("zb%d" % c), K("xl", 0, NJ)), F.Copy)
-        act(K("nx"), ind(R("nt"), K("sl", 0, NJ)), F.Copy)
+        act(K("nx"), ind(R("nt"), K("xl", NJ, 2 * NJ)), F.Copy)
         ts(K("hx"), K("zx"), 0.0, A.is_ge)
         b = bank(c)
         mm([(R(b, 0, LC), R("eye"), K("zx"), True, False), (R(b, 0, LC), R("i512"), K("hx"), False, False), (R(b, 0, LC), R("eye"), K("nx"), False, True)])
-        act(K("w8"), R(b, 0, LC), F.Exp, R("m1c", 1, 2), LN2)
+        act(K("w8"), R(b, 0, LC), F.Exp, BC["w8"], LN2)
         ts(K("f1"), K("w8"), 0.0, A.is_gt)
         b = bank(c)
         mm([(R(b, 0, LC), R("blk"), K("w8"), True, True)])
@@ -420,10 +433,10 @@ def rank_program(g, core, T, topo):
         act(K("D"), R(b, 0, LC), F.Relu)
         tt(K("ds"), K("D"), S_, A.mult)
         b = bank(c)
-        pw = wbank(c)
-        mm([(R(b, 0, LC), R("blk"), K("xs"), True, False), (R(b, 0, LC), R("i2048"), R("ones", 0, LC), False, True),
+        mm([(R(b, 0, LC), R("blk"), K("xq", LC, 2 * LC), True, False), (R(b, 0, LC), R("i2048"), R("ones", 0, LC), False, True),
             (R(b, LC, 2 * LC), R("blk"), K("ds"), True, False), (R(b, LC, 2 * LC), R("i2048"), R("ones", 0, LC), False, True)])
-        mm([(R(pw, 2 * LC, 3 * LC), R("blk"), K("ds"), True, False), (R(pw, 2 * LC, 3 * LC), R("eye"), R("ones", 0, LC), False, True)])
+        mm([(R(pw, 2 * LC, 3 * LC), R("blk"), K("ds"), True, False), (R(pw, 2 * LC, 3 * LC), R("eye"), R("ones", 0, LC), False, True),
+            (wp, R("eye"), R(w, 0, 2 * LC), True, True)])
         act(K("sx"), R(b, 0, LC), F.Copy)
         act(R(b, 2 * LC, 3 * LC), R(b, 0, LC), F.Copy, float(97 * t), R("kap", 0, 1))
         tt(K("pr"), R(b, LC, 2 * LC), K("sx"), A.mult)
@@ -431,110 +444,89 @@ def rank_program(g, core, T, topo):
         tt(K("sm"), K("sh"), R(b, 2 * LC, 3 * LC), A.add)
         ts(K("ci"), K("sm"), 4095, A.bitwise_and)
         cp(K("c16"), K("ci"))
+        PH[0] = "net%d" % c
+
+        def prod(n, wd, mask):
+            tt(K(n, 0, LC), R(wd[0], wd[1], wd[1] + LC), mask, A.mult)
+            tt(K(n, LC, 2 * LC), R(wd[0], wd[1] + LC, wd[1] + 2 * LC), mask, A.mult)
         ts(K("cf"), K("ci"), -2048.0, A.add)
         tt(K("qe"), Q_, R(pw, 2 * LC, 3 * LC), A.is_equal)
-        act(R("cg%d" % c), ind(R("gt"), K("c16")), F.Copy)
-        b = bank(c)
-        mm([(R(b, 0, LC), R("im85"), K("hx"), True, False), (R(b, 0, LC), R("eye"), K("nx"), False, True)])
-        hb, cg = "hb%d" % c, "cg%d" % c
-        for m in range(16 - MACT):
-            tt(R(hb, m * LC, (m + 1) * LC), R(cg, m, CA, 16), R(b, 0, LC), A.is_gt)
-        for m0 in range(16 - MACT, 16, 512 // LC):
-            b = bank(c)
-            k = min(512 // LC, 16 - m0)
-            it = []
-            for m in range(m0, m0 + k):
-                o = R(b, (m - m0) * LC, (m - m0 + 1) * LC)
-                it += [(o, R("eye"), R(cg, m, CA, 16), True, False), (o, R("i85"), K("hx"), False, False), (o, R("neg"), K("nx"), False, True)]
-            mm(it)
-            act(R(hb, m0 * LC, (m0 + k) * LC), R(b, 0, k * LC), F.Sign)
-        b = bank(c)
-        mm([(R(b, 0, LC), R("wk" if m < 16 - MACT else "wh", 128 * m, 128 * m + 128), R(hb, m * LC, (m + 1) * LC), m == 0, m == 15) for m in range(16)])
-        act(K("pw"), R(b, 0, LC), F.Exp, R("pb", 0, 1), 5.0 * LN2)
-        b = bank(c)
-        mm([(R(b, 0, LC), R("nblk"), K("f1"), True, False), (R(b, 0, LC), R("eye"), R("bark", c * LC, (c + 1) * LC), False, True)])
-        act(K("tb"), R(b, 0, LC), F.Exp, R("m1c", 2, 3), 5.0 * LN2)
-        b = bank(c)
-        mm([(R(b, 0, LC), R("blkz"), K("pw"), True, True)])
-        tt(K("eq"), R(b, 0, LC), K("pw"), A.is_le)
-        tt(K("insi"), R(b, 0, LC), K("tb"), A.is_ge)
-        b = bank(c)
-        mm([(R(b, 0, LC), R("first"), K("eq"), True, True),
-            (R(b, LC, 2 * LC), R("blk"), K("X"), True, False), (R(b, LC, 2 * LC), R("neg"), K("insi"), False, True),
-            (R(b, 2 * LC, 3 * LC), R("tri"), K("X"), True, False), (R(b, 2 * LC, 3 * LC), R("eye"), K("insi"), False, True),
-            (R(b, 3 * LC, 4 * LC), R("eye"), K("X"), True, False), (R(b, 3 * LC, 4 * LC), R("eye"), K("insi"), False, True)])
-        act(K("ret"), R(b, LC, 2 * LC), F.Relu, accum=R("ac%d_%d" % (t, c), 0, 1))
-        act(K("M"), R(b, 0, LC), F.Relu)
-        ts(K("mi"), R(b, 2 * LC, 3 * LC), -1.0, A.add, 0.0, A.max)
-        ts(K("xi"), R(b, 3 * LC, 4 * LC), -1.0, A.add, 0.0, A.max)
-        tt(K("mc"), K("M"), K("cf"), A.mult)
-        mm([(R(pw, 3 * LC, 4 * LC), R("blk"), K("mc"), True, True)])
-        tt(K("iv", 0, LC), K("xi"), R(pw, 3 * LC, 4 * LC), A.mult)
-        tt(K("iv", LC, 2 * LC), K("xi"), R(pw, 2 * LC, 3 * LC), A.mult)
-        b = bank(c)
-        mm([(R(b, 0, LC), R("eye"), K("D"), True, False), (R(b, 0, LC), R("eye"), K("qe"), False, False), (R(b, 0, LC), R("i4"), K("ret"), False, True)])
-        ts(K("go"), R(b, 0, LC), 4.5, A.is_ge)
-        b = bank(c)
-        mm([(R(b, 0, LC), R("blk"), K("go"), True, True), (R(b, LC, 2 * LC), R("mr"), K("go"), True, True)])
-        act(K("rb"), R(b, LC, 2 * LC), F.Relu)
-        ts(K("fm"), R(b, 0, LC), R("k16", 0, 1), A.is_ge)
-        pr = R(b, LC, 2 * LC)
-        wp = R(pw, 0, 2 * LC)
-        wS, wQ = R(pw, 0, LC), R(pw, LC, 2 * LC)
-        mm([(wp, R("eye"), R(w, 0, 2 * LC), True, True)])
-
-        def prod(n, mask):
-            tt(K(n, 0, LC), wS, mask, A.mult)
-            tt(K(n, LC, 2 * LC), wQ, mask, A.mult)
-        prod("a1", K("mi"))
-        prod("a2", K("go"))
+        o = R(nb, 0, LC)
+        mm([(o, R("eye"), K("D"), True, False), (o, R("eye"), K("qe"), False, False), (o, R("blk4"), K("X"), False, True)])
+        ts(K("go"), o, 4.5, A.is_ge)
+        pr = R(nb, LC, 2 * LC)
+        mm([(o, R("blk"), K("go"), True, True), (pr, R("mr"), K("go"), True, True)])
+        act(K("rb"), pr, F.Relu)
+        ts(K("fm"), o, R("k16", 0, 1), A.is_ge)
+        prod("a2", wp, K("go"))
         tt(K("fi", 0, LC), K("fm"), K("cf"), A.mult)
         ts(K("fi", LC, 2 * LC), K("fm"), -2048.0, A.mult)
-        base, moves = R(w, 0, 2 * LC), [("shd", "a1"), ("neg", "a2")]
+        base, moves = R(w, 0, 2 * LC), [("neg", "a2")]
         for s in range(4):
             ts(K("ri"), pr, 0.0, A.max)
             ts(K("mk"), K("ri"), s, A.arith_shift_right, 1, A.bitwise_and)
-            prod("m%d" % s, K("mk"))
+            prod("m%d" % s, wp, K("mk"))
             moves.append(("sh%d" % (1 << s), "m%d" % s))
             if s < 3:
                 tt(K("ar"), pr, K("mk"), A.mult)
-                b = bank(c)
-                pr2 = R(b, 0, LC)
-                mm([(pr2, R("eye"), K("rb"), True, False), (pr2, R("sh%d" % (1 << s)), K("ar"), False, True)])
-                pr = pr2
+                pr = R(nb, ((s + 2) % 4) * LC, ((s + 2) % 4 + 1) * LC)
+                mm([(pr, R("eye"), K("rb"), True, False), (pr, R("sh%d" % (1 << s)), K("ar"), False, True)])
                 if s < 2:
                     act(K("rb"), pr, F.Copy)
             if s == 3:
-                moves += [("eye", "iv"), ("eye", "fi")]
+                moves += [("eye", "fi")]
             mm([(wp, R("eye"), base, True, False)] + [(wp, R(m), K(a), False, q == len(moves) - 1) for q, (m, a) in enumerate(moves)])
             if s == 1:
                 cp(K("wb"), wp)
                 base, moves = K("wb"), []
+        mm([(n2, R("eye"), R(w, 0, 2 * LC), True, True)])
+        PH[0] = "score%d" % c
+        hb, cg = "hb%d" % c, "cg%d" % c
+        rb_ = bank(c)
+        rr = R(rb_, 0, LC)
+        mm([(rr, R("im85"), K("hx"), True, False), (rr, R("eye"), K("nx"), False, True)])
+        b = bank(c)
+        mm([(R(b, 0, LC), R("nblk"), K("f1"), True, False), (R(b, 0, LC), R("eye"), R("bark", c * LC, (c + 1) * LC), False, True)])
+        act(K("tb"), R(b, 0, LC), F.Exp, BC["tb"], 5.0 * LN2)
+        act(R(cg), ind(R("gt"), K("c16")), F.Copy)
+        for m in range(16):
+            tt(R(hb, m * LC, (m + 1) * LC), R(cg, m, CA, 16), rr, A.is_gt)
+        mm([(R(b, m, 128, 16), R(hb, m * LC, (m + 1) * LC), R("blk", 0, 128, 16), True, True) for m in range(16)])
+        act(K("pv"), R(b, 0, LC), F.Exp, BC["pv"], 5.0 * LN2)
+        mm([(R(b, LC, 2 * LC), K("pv"), R("eye"), True, True)])
+        act(K("pw"), R(b, LC, 2 * LC), F.Copy)
+        mm([(rr, R("blkz"), K("pw"), True, True)])
+        tt(K("eq"), rr, K("pw"), A.is_le)
+        tt(K("insi"), rr, K("tb"), A.is_ge)
+        tt(K("nin"), rr, K("tb"), A.is_lt)
+        b = bank(c)
+        mm([(R(b, 0, LC), R("first"), K("eq"), True, True)])
+        act(K("M"), R(b, 0, LC), F.Relu)
+        mm([(R(b, LC, 2 * LC), R("tri"), K("X"), True, False), (R(b, LC, 2 * LC), R("eye"), K("insi"), False, True),
+            (R(b, 2 * LC, 3 * LC), R("eye"), K("X"), True, False), (R(b, 2 * LC, 3 * LC), R("eye"), K("insi"), False, True),
+            (R(b, 3 * LC, 4 * LC), R("blk"), K("X"), True, False), (R(b, 3 * LC, 4 * LC), R("neg"), K("insi"), False, True)])
+        act(K("mi"), R(b, LC, 2 * LC), F.Relu, BC["one"])
+        act(K("xi"), R(b, 2 * LC, 3 * LC), F.Relu, BC["one"])
+        if t < VI - 1:
+            act(K("ret"), R(b, 3 * LC, 4 * LC), F.Relu, accum=R("ac%d_%d" % (t, c), 0, 1))
+        tt(K("mc"), K("M"), K("cf"), A.mult)
+        mm([(rr, R("blk"), K("mc"), True, True)])
+        PH[0] = "fin%d" % c
+        prod("a1", n2, K("mi"))
+        prod("m0", n2, K("insi"))
+        prod("m1", wp, K("nin"))
+        tt(K("iv", LC, 2 * LC), K("xi"), R(pw, 2 * LC, 3 * LC), A.mult)
+        tt(K("iv", 0, LC), K("xi"), rr, A.mult)
+        b = bank(c)
+        fp = R(b, 0, 2 * LC)
+        mm([(fp, R("eye"), K("m1"), True, False), (fp, R("eye"), K("m0"), False, False), (fp, R("shd"), K("a1"), False, False), (fp, R("eye"), K("iv"), False, True)])
         if t < VI - 1:
             wo = "wo%d_%d" % (t, c)
-            cp(R(wo), wp)
+            cp(R(wo), fp)
             remote("p%d_%d" % (t, c), R("w%d_%d" % (t + 1, c)), R(wo))
         else:
-            act(R("ysk", c * LC, (c + 1) * LC), wS, F.Copy, 2048.0)
-            act(R("ywk", c * LC, (c + 1) * LC), wQ, F.Copy, 2047.0)
-
-    def table(t, c):
-        def K(n, *a):
-            return R("%s_%d" % (n, c), *a)
-        p = lists(c, "wk", "val_%d" % c)
-        cp(K("ui"), p)
-        ts(K("uj"), K("ui"), 15, A.bitwise_and)
-        tt(K("uk"), K("uj"), K("vb"), A.add)
-        cp(K("vl", 0, NJ), K("uk"))
-        act(K("eo"), ind(R("er"), K("vl", 0, NJ)), F.Copy)
-        tt(K("es"), K("eo"), K("val"), A.add)
-        ts(K("eh"), K("es"), 1, A.arith_shift_right)
-        cp(K("ne"), K("eh"))
-        if t < VI - 1:
-            code(K("ng"), K("ne"), K("cl"), K("hh"), c, LC)
-        cp(ind(R("er"), K("vl", 0, NJ)), K("ne"))
-        if t < VI - 1:
-            cp(ind(R("gt"), K("vl", 0, NJ)), K("ng"))
+            act(R("ysk", c * LC, (c + 1) * LC), R(b, 0, LC), F.Copy, 2048.0)
+            act(R("ywk", c * LC, (c + 1) * LC), R(b, LC, 2 * LC), F.Copy, 2047.0)
 
     def count(t):
         b = bank(0)
@@ -559,7 +551,7 @@ def rank_program(g, core, T, topo):
         dma("a", R("yw", 16 * k, 16 * k + 16), R("ywk", None, None, 1, (k, 128, 16)))
 
     n = len(ops)
-    HOP = 0.12
+    HOP = 0.07
     tail = [0.0] * n
     succ = [[] for _ in range(n)]
     for i, o in enumerate(ops):
@@ -571,6 +563,7 @@ def rank_program(g, core, T, topo):
         for j in succ[i]:
             m = max(m, tail[j])
         tail[i] = m + o["cost"] + o["lat"] + HOP
+    prio = [tail[i] + BIAS.get(ops[i]["ph"], 0.0) for i in range(n)]
     ndep = [len(o["deps"]) for o in ops]
     ready = [0.0] * n
     avail = [i for i in range(n) if ndep[i] == 0]
@@ -581,7 +574,7 @@ def rank_program(g, core, T, topo):
         for i in avail:
             q = ops[i]["q"]
             st = ready[i] if q == "x" else max(ready[i], free[q])
-            key = (round(st, 2), -tail[i], i)
+            key = (round(st, 2), -prio[i], i)
             if best is None or key < best[0]:
                 best = (key, i, st)
         _, i, st = best
@@ -614,7 +607,7 @@ def rank_program(g, core, T, topo):
             done[i] = (o["sem"], o["inc"], {o["sem"]: o["inc"]})
             tot[o["sem"]] = o["inc"]
             continue
-        for d in sorted(o["deps"], key=lambda d: -order.index(d) if False else d, reverse=True):
+        for d in sorted(o["deps"], reverse=True):
             sem, v, clk = done[d]
             if known[q].get(sem, 0) < v:
                 wait(q, sem, v)
@@ -624,20 +617,14 @@ def rank_program(g, core, T, topo):
         for f in o["fns"]:
             r = f()
             if o["kind"] == "c":
-                s = QS[q]
-                cnt[s] += 1
-                r.then_inc(T.sem[s], 1)
+                cnt[QS[q]] += 1
+                r.then_inc(T.sem[QS[q]], 1)
             elif o["kind"] == "d":
                 r.then_inc(T.sem[o["sem"]], 16)
         clk = dict(known[q])
-        if o["kind"] == "c":
-            s = QS[q]
-            clk[s] = cnt[s]
-            done[i] = (s, cnt[s], clk)
-            tot[s] = cnt[s]
-        else:
-            clk[o["sem"]] = o["inc"]
-            done[i] = (o["sem"], o["inc"], clk)
-            tot[o["sem"]] = o["inc"]
+        s, v = (QS[q], cnt[QS[q]]) if o["kind"] == "c" else (o["sem"], o["inc"])
+        clk[s] = v
+        done[i] = (s, v, clk)
+        tot[s] = v
     for s, v in tot.items():
         wait("g", s, v)

@@ -12,8 +12,9 @@ LN2 = math.log(2.0)
 BIG = 1024.0
 NDMA = 80
 NB = 8 // NCH
-BIAS = {"run0": 2.8, "end0": -2.9, "head0": 8.4, "net0": 6.9, "score0": 7.1, "fin0": 10.8, "fin1": -3.5, "run1": -9.1,
-        "net1": -3.7, "head1": 2.9, "score1": -2.5, "end1": -2.0, "tab": -10.2}
+BIAS = {"run0": -2.3, "end0": -1.5, "head0": 5.7, "net0": 6.6, "score0": 7.1, "fin0": 6.9, "fin1": -8.9, "run1": -8.5,
+        "net1": -4.1, "head1": 2.0, "score1": -2.5, "end1": -1.2, "tab": -3.6}
+ND = 2
 
 SCRATCH = {}
 SEMAPHORES = ["qv", "qa", "qt", "qg"] + ["d%d" % i for i in range(NDMA)]
@@ -40,10 +41,9 @@ for _n in ("er", "gt", "nt", "tq"):
 for _n in ("ip", "ic", "gp", "gc", "kp", "kc"):
     _buf(_n, 128, "int32")
 for _n in ("dd", "cc", "pp", "ns", "eye", "blk", "str", "tri", "first", "half", "shd", "sh1", "sh2", "sh4", "sh8", "neg",
-           "i4", "im85", "i512", "i71", "i72", "i2048", "mt", "mth", "mr", "blkz", "ones", "nblk", "blk4"):
+           "i4", "im85", "i512", "i71", "i72", "i2048", "mt", "mth", "mr", "blkz", "ones", "nblk", "blk4", "e0"):
     _buf(_n, 128, "bfloat16")
-for _n in ("wk", "br"):
-    _buf(_n, 16 * 128, "bfloat16")
+_buf("wk", 16 * 128, "bfloat16")
 _buf("thf", 128, "float32")
 _buf("allo", 128, "float32")
 for _n in ("kcol", "kap", "cq", "k16", "thr", "m1c"):
@@ -51,8 +51,8 @@ for _n in ("kcol", "kap", "cq", "k16", "thr", "m1c"):
 _buf("rci", 8, "int32")
 _buf("xbase", 2 * NJ, "bfloat16")
 _buf("xbi", NJ, "int32")
-_buf("barl", 16, "int32")
-_buf("barb", 16, "bfloat16")
+_buf("bari", 256, "int32")
+_buf("barb", 256, "bfloat16")
 for _n in ("bark", "sti", "sth", "stc"):
     _buf(_n, 256, "bfloat16")
 _buf("actk", 256, "int32")
@@ -70,11 +70,11 @@ for _c in range(NCH):
     for _n in ("kb", "zb", "fl", "cg", "hb"):
         _buf("%s%d" % (_n, _c), CA, "bfloat16")
     for _n in ("e15", "k15", "t15", "val", "h8", "ov", "X", "zx", "nx", "hx", "w8", "f1", "T", "D", "pw", "pv", "eq", "M",
-               "insi", "nin", "mi", "xi", "ret", "qe", "go", "fm", "rb", "ar", "eo", "ne", "cl", "hh", "ng"):
+               "insi", "nin", "xi", "ret", "qe", "go", "fm", "rb", "ar", "eo", "ne", "cl", "hh", "ng"):
         _buf("%s_%d" % (_n, _c), LC, "bfloat16")
-    for _n in ("ds", "cf", "mc"):
+    for _n in ("ds", "cf", "mc", "iv", "iq"):
         _buf("%s_%d" % (_n, _c), LC, "float16")
-    for _n in ("a1", "a2", "m0", "m1", "m2", "m3", "wb", "iv", "fi", "xq"):
+    for _n in ("a1", "a2", "m0", "m1", "m2", "m3", "wb", "fi", "xq"):
         _buf("%s_%d" % (_n, _c), 2 * LC, "float16")
     for _n in ("f4", "y7", "pr", "sh", "sm", "ci", "ri", "mk", "eh"):
         _buf("%s_%d" % (_n, _c), LC, "int32")
@@ -249,15 +249,19 @@ def rank_program(g, core, T, topo):
     def wbank(c):
         return "p%d" % (c * NB + NB - 1)
 
+    def lanes(q, buf, name, r0, r1):
+        for r in range(r0, r1):
+            dma(q, R(buf, 16 * r, 16 * r + 16), R(name, None, None, 1, (r, 128, 16)))
     for j in range(4):
-        c0, c1 = j * 1024, (j + 1) * 1024
-        dma("s", R("er", c0, c1), R("eff", c0, c1))
-        dma("a", R("tq", c0, c1), R("req", c0, c1))
+        dma("s", R("er", 1024 * j, 1024 * j + 1024), R("eff", 1024 * j, 1024 * j + 1024))
+    lanes("a", "actk", "act", 0, 16 // NCH)
     dma("a", R("sti"), R("st0"))
-    dma("s", R("barl"), R("bar"))
-    for k in range(16):
-        dma("s", R("actk", None, None, 1, (k, 128, 16)), R("act", 16 * k, 16 * k + 16))
-        dma("a", R("whyk", None, None, 1, (k, 128, 16)), R("why", 16 * k, 16 * k + 16))
+    for j in range(4):
+        dma("s", R("tq", 1024 * j, 1024 * j + 1024), R("req", 1024 * j, 1024 * j + 1024))
+    lanes("s", "actk", "act", 16 // NCH, 16)
+    fill(R("bari"), 0)
+    dma("s", R("bari", None, None, 1, (0, 128, 16)), R("bar"))
+    lanes("s", "whyk", "why", 0, 16)
 
     def iota(out, pattern, base, cm):
         add("g", [lambda: g.iota(x(out), pattern, base, cm)], [], [out], 0.13 + 2 * n_of(out) * CY)
@@ -288,9 +292,9 @@ def rank_program(g, core, T, topo):
     ts(R("half"), R("first"), 0.5, A.mult)
     ts(R("mr"), R("eye"), -64.0, A.mult)
     tt(R("mr"), R("mr"), R("str"), A.add)
-    ts(R("hb0", 0, 128), R("pp"), 0.0, A.is_equal)
+    ts(R("e0"), R("pp"), 0.0, A.is_equal)
     ts(R("mt"), R("sh1"), -2.0, A.mult)
-    tt(R("mt"), R("mt"), R("hb0", 0, 128), A.subtract)
+    tt(R("mt"), R("mt"), R("e0"), A.subtract)
     ts(R("thf"), R("dd"), 5.0, A.min, 8.0 * LN2, A.mult)
     ts(R("kcol", 0, 1), R("kp", 0, 1), 1.0, A.mult)
     BC = {}
@@ -304,8 +308,9 @@ def rank_program(g, core, T, topo):
     ts(R("nblk"), R("blk"), -1.0, A.mult)
     for k in range(16):
         ts(R("wk", 128 * k, 128 * k + 128), R("cc"), float(k), A.is_equal)
-        ts(R("br", 128 * k, 128 * k + 128), R("pp"), float(k), A.is_equal)
-    ts(R("kap", 0, 1), R("kcol", 0, 1), 241.0, A.mult, 37.0, A.add)
+    ts(R("kap", 0, 1), R("kcol", 0, 1), 241.0, A.mult, 101.0, A.add)
+    for t in range(VI):
+        ts(R("kap", 4 + t, 5 + t), R("kap", 0, 1), 2048.0, A.mult, float(97 * t), A.add)
     ts(R("cq", 0, 1), R("kcol", 0, 1), -16.0, A.mult, 0.5, A.add)
     ts(R("k16", 0, 1), R("kcol", 0, 1), -1.0, A.mult, 16.0, A.add)
     fill(R("thr", 0, 1), -1.5)
@@ -317,9 +322,9 @@ def rank_program(g, core, T, topo):
     ts(R("kcol", 4, 5), R("kcol", 0, 1), 256.0, A.mult)
     for c in range(NCH):
         ts(R("vb_%d" % c), R("vb_%d" % c), R("kcol", 4, 5), A.add)
-    cp(R("barb"), R("barl"))
+    cp(R("barb"), R("bari"))
     b = bank(0)
-    mm([(R(b, 16 * r, 16 * r + 16), R("br", 128 * r, 128 * r + 128), R("barb"), True, True) for r in range(16)])
+    mm([(R(b, 0, 256), R("e0"), R("barb"), True, True)])
     cp(R("bark"), R(b, 0, 256))
     for c in range(NCH):
         a0, a1 = c * LC, (c + 1) * LC
@@ -329,7 +334,7 @@ def rank_program(g, core, T, topo):
     tt(R("stc"), R("sti"), R("sth"), A.add)
     for r in range(16):
         c, o = divmod(16 * r, LC)
-        ts(R("s0_%d" % c, o, o + 16), R("stc", r, 256, 16), -20.0, A.add)
+        act(R("s0_%d" % c, o, o + 16), R("stc", r, 256, 16), F.Copy, -20.0)
 
     def code(dst, src, cl, hh, b, n):
         ts(cl, src, 4.0, A.max, 11.0, A.min)
@@ -339,6 +344,14 @@ def rank_program(g, core, T, topo):
     for j in range(8):
         c0, c1 = 512 * j, 512 * j + 512
         d = 512 * (j % 4)
+        if j >= 8 - ND:
+            n1, n2 = R("fl%d" % (j % 2), d, d + 512), R("cg%d" % (j % 2), d, d + 512)
+            ts(n1, R("er", c0, c1), 4.0, A.max, 11.0, A.min)
+            tt(n2, R("er", c0, c1), n1, A.subtract)
+            ts(n1, R("er", c0, c1), 12.0, A.is_ge, 143.0, A.mult)
+            tt(n2, n2, n1, A.add)
+            ts(R("gt", c0, c1), n2, -8.0, A.add)
+            continue
         code(R("gt", c0, c1), R("er", c0, c1), R("kb%d" % (j // 4), d, d + 512), R("zb%d" % (j // 4), d, d + 512), bank(j % 2), 512)
     for j in range(4):
         c0, c1 = 1024 * j, 1024 * j + 1024
@@ -406,11 +419,13 @@ def rank_program(g, core, T, topo):
         S_, Q_ = R(w, 0, LC), R(w, LC, 2 * LC)
         pw, nb = wbank(c), nbank(c)
         wp, n2 = R(pw, 0, 2 * LC), R(nb, 0, 2 * LC)
+        mm([(wp, R("eye"), R(w, 0, 2 * LC), True, True)])
+        wS = R(pw, 0, LC)
         b = bank(c)
         mm([(R(b, 0, LC), R("half"), K("ov"), True, True)])
         act(K("X"), R(b, 0, LC), F.Relu, R("cq", 0, 1))
         ts(K("xq", 0, LC), K("X"), R("kcol", 0, 1), A.mult)
-        tt(K("xq", LC, 2 * LC), K("X"), S_, A.mult)
+        tt(K("xq", LC, 2 * LC), K("X"), wS, A.mult)
         b = bank(c)
         mm([(R(b, 0, 2 * NJ), R("wk", 128 * r, 128 * r + 128), R("xq_%d" % c, r, 2 * LC, 16), r == 0, False) for r in range(16)]
            + [(R(b, 0, 2 * NJ), R("eye"), R("xbase"), False, True)])
@@ -431,14 +446,13 @@ def rank_program(g, core, T, topo):
         b = bank(c)
         mm([(R(b, 0, LC), R("mt"), K("T"), True, False), (R(b, 0, LC), R("eye"), K("X"), False, True)])
         act(K("D"), R(b, 0, LC), F.Relu)
-        tt(K("ds"), K("D"), S_, A.mult)
+        tt(K("ds"), K("D"), wS, A.mult)
         b = bank(c)
-        mm([(R(b, 0, LC), R("blk"), K("xq", LC, 2 * LC), True, False), (R(b, 0, LC), R("i2048"), R("ones", 0, LC), False, True),
-            (R(b, LC, 2 * LC), R("blk"), K("ds"), True, False), (R(b, LC, 2 * LC), R("i2048"), R("ones", 0, LC), False, True)])
-        mm([(R(pw, 2 * LC, 3 * LC), R("blk"), K("ds"), True, False), (R(pw, 2 * LC, 3 * LC), R("eye"), R("ones", 0, LC), False, True),
-            (wp, R("eye"), R(w, 0, 2 * LC), True, True)])
-        act(K("sx"), R(b, 0, LC), F.Copy)
-        act(R(b, 2 * LC, 3 * LC), R(b, 0, LC), F.Copy, float(97 * t), R("kap", 0, 1))
+        mm([(R(b, 0, LC), R("blk"), K("xq", LC, 2 * LC), True, True)])
+        mm([(R(b, LC, 2 * LC), R("blk"), K("ds"), True, True)])
+        mm([(R(pw, 2 * LC, 3 * LC), R("blk"), K("ds"), True, False), (R(pw, 2 * LC, 3 * LC), R("eye"), R("ones", 0, LC), False, True)])
+        act(K("sx"), R(b, 0, LC), F.Copy, 2048.0)
+        act(R(b, 2 * LC, 3 * LC), R(b, 0, LC), F.Copy, R("kap", 4 + t, 5 + t), R("kap", 0, 1))
         tt(K("pr"), R(b, LC, 2 * LC), K("sx"), A.mult)
         ts(K("sh"), K("pr"), 5, A.arith_shift_right)
         tt(K("sm"), K("sh"), R(b, 2 * LC, 3 * LC), A.add)
@@ -458,6 +472,11 @@ def rank_program(g, core, T, topo):
         mm([(o, R("blk"), K("go"), True, True), (pr, R("mr"), K("go"), True, True)])
         act(K("rb"), pr, F.Relu)
         ts(K("fm"), o, R("k16", 0, 1), A.is_ge)
+        o2 = R(nb, 2 * LC, 3 * LC)
+        mm([(o2, R("tri"), K("X"), True, True)])
+        tt(K("a1", 0, LC), S_, o2, A.mult)
+        tt(K("a1", LC, 2 * LC), Q_, o2, A.mult)
+        tt(K("iq"), K("X"), R(pw, 2 * LC, 3 * LC), A.mult)
         prod("a2", wp, K("go"))
         tt(K("fi", 0, LC), K("fm"), K("cf"), A.mult)
         ts(K("fi", LC, 2 * LC), K("fm"), -2048.0, A.mult)
@@ -479,7 +498,8 @@ def rank_program(g, core, T, topo):
             if s == 1:
                 cp(K("wb"), wp)
                 base, moves = K("wb"), []
-        mm([(n2, R("eye"), R(w, 0, 2 * LC), True, True)])
+        mm([(n2, R("eye"), R(w, 0, 2 * LC), True, False), (n2, R("shd"), K("a1"), False, False),
+            (R(nb, LC, 2 * LC), R("eye"), K("iq"), False, True)])
         PH[0] = "score%d" % c
         hb, cg = "hb%d" % c, "cg%d" % c
         rb_ = bank(c)
@@ -502,24 +522,20 @@ def rank_program(g, core, T, topo):
         b = bank(c)
         mm([(R(b, 0, LC), R("first"), K("eq"), True, True)])
         act(K("M"), R(b, 0, LC), F.Relu)
-        mm([(R(b, LC, 2 * LC), R("tri"), K("X"), True, False), (R(b, LC, 2 * LC), R("eye"), K("insi"), False, True),
-            (R(b, 2 * LC, 3 * LC), R("eye"), K("X"), True, False), (R(b, 2 * LC, 3 * LC), R("eye"), K("insi"), False, True),
+        mm([(R(b, 2 * LC, 3 * LC), R("eye"), K("X"), True, False), (R(b, 2 * LC, 3 * LC), R("eye"), K("insi"), False, True),
             (R(b, 3 * LC, 4 * LC), R("blk"), K("X"), True, False), (R(b, 3 * LC, 4 * LC), R("neg"), K("insi"), False, True)])
-        act(K("mi"), R(b, LC, 2 * LC), F.Relu, BC["one"])
         act(K("xi"), R(b, 2 * LC, 3 * LC), F.Relu, BC["one"])
         if t < VI - 1:
             act(K("ret"), R(b, 3 * LC, 4 * LC), F.Relu, accum=R("ac%d_%d" % (t, c), 0, 1))
         tt(K("mc"), K("M"), K("cf"), A.mult)
         mm([(rr, R("blk"), K("mc"), True, True)])
         PH[0] = "fin%d" % c
-        prod("a1", n2, K("mi"))
         prod("m0", n2, K("insi"))
         prod("m1", wp, K("nin"))
-        tt(K("iv", LC, 2 * LC), K("xi"), R(pw, 2 * LC, 3 * LC), A.mult)
-        tt(K("iv", 0, LC), K("xi"), rr, A.mult)
+        tt(K("iv"), K("xi"), rr, A.mult)
         b = bank(c)
         fp = R(b, 0, 2 * LC)
-        mm([(fp, R("eye"), K("m1"), True, False), (fp, R("eye"), K("m0"), False, False), (fp, R("shd"), K("a1"), False, False), (fp, R("eye"), K("iv"), False, True)])
+        mm([(fp, R("eye"), K("m1"), True, False), (fp, R("eye"), K("m0"), False, False), (R(b, 0, LC), R("eye"), K("iv"), False, True)])
         if t < VI - 1:
             wo = "wo%d_%d" % (t, c)
             cp(R(wo), fp)
@@ -527,6 +543,9 @@ def rank_program(g, core, T, topo):
         else:
             act(R("ysk", c * LC, (c + 1) * LC), R(b, 0, LC), F.Copy, 2048.0)
             act(R("ywk", c * LC, (c + 1) * LC), R(b, LC, 2 * LC), F.Copy, 2047.0)
+            for r in range(c * NJ, (c + 1) * NJ):
+                dma("s", R("ys", None, None, 1, (r, 128, 16)), R("ysk", 16 * r, 16 * r + 16))
+                dma("a" if c == NCH - 1 else "s", R("yw", None, None, 1, (r, 128, 16)), R("ywk", 16 * r, 16 * r + 16))
 
     def count(t):
         b = bank(0)
@@ -546,9 +565,6 @@ def rank_program(g, core, T, topo):
             count(t)
     for j in range(2):
         dma("s" if j else "a", R("ye", 2048 * j, 2048 * j + 2048), R("er", 2048 * j, 2048 * j + 2048))
-    for k in range(16):
-        dma("s", R("ys", 16 * k, 16 * k + 16), R("ysk", None, None, 1, (k, 128, 16)))
-        dma("a", R("yw", 16 * k, 16 * k + 16), R("ywk", None, None, 1, (k, 128, 16)))
 
     n = len(ops)
     HOP = 0.07

import numpy as np
import math
import comms_topo
from concourse.mybir import AluOpType as A, ActivationFunctionType as F

NCH, W, L, VI = 2, 4096, 16, 4
LC = 256 // NCH
CA = LC * L
NJ = LC // 16
NP = 2
LN2 = math.log(2.0)
BIG = 1024.0
NDMA = 80
NB = 8 // NCH
BIAS = {"run0": -2.3, "end0": -1.5, "head0": 5.7, "net0": 6.6, "score0": 7.1, "fin0": 6.9, "fin1": -8.9, "run1": -8.5,
        "net1": -4.1, "head1": 2.0, "score1": -2.5, "end1": -1.2, "tab": -3.6}
ND = 2

SCRATCH = {}
SEMAPHORES = ["qv", "qa", "qt", "qg"] + ["d%d" % i for i in range(NDMA)]
for _t in range(VI - 1):
    for _c in range(NCH):
        SEMAPHORES += ["ap%d_%d" % (_t, _c), "as%d_%d" % (_t, _c), "lp%d_%d" % (_t, _c), "ls%d_%d" % (_t, _c)]
LOG = {}
_SHORT = {"bfloat16": "bf", "float16": "hf", "float32": "ff", "int32": "nn", "uint16": "uu"}


def _buf(name, cols, dtype, where="sbuf"):
    if where == "psum":
        SCRATCH[name] = (where, [128, cols], dtype)
        LOG[name] = (where, cols, dtype, name, 0)
        return
    t = "pk" + _SHORT[dtype]
    o = SCRATCH[t][1][1] if t in SCRATCH else 0
    SCRATCH[t] = ("sbuf", [128, o + -(-cols // 64) * 64], dtype)
    LOG[name] = (where, cols, dtype, t, o)


for _n in ("er", "gt", "nt", "tq"):
    _buf(_n, W, "bfloat16")
for _n in ("ip", "ic", "gp", "gc", "kp", "kc"):
    _buf(_n, 128, "int32")
for _n in ("dd", "cc", "pp", "ns", "eye", "blk", "str", "tri", "first", "half", "shd", "sh1", "sh2", "sh4", "sh8", "neg",
           "i4", "im85", "i512", "i71", "i72", "i2048", "mt", "mth", "mr", "blkz", "ones", "nblk", "blk4", "e0"):
    _buf(_n, 128, "bfloat16")
_buf("wk", 16 * 128, "bfloat16")
_buf("thf", 128, "float32")
_buf("allo", 128, "float32")
for _n in ("kcol", "kap", "cq", "k16", "thr", "m1c"):
    _buf(_n, 8, "float32")
_buf("rci", 8, "int32")
_buf("xbase", 2 * NJ, "bfloat16")
_buf("xbi", NJ, "int32")
_buf("bari", 256, "int32")
_buf("barb", 256, "bfloat16")
for _n in ("bark", "sti", "sth", "stc"):
    _buf(_n, 256, "bfloat16")
_buf("actk", 256, "int32")
_buf("whyk", 256, "int32")
_buf("ysk", 256, "float32")
_buf("ywk", 256, "float32")
for _c in range(NCH):
    for _t in range(VI):
        _buf("w%d_%d" % (_t, _c), 2 * LC, "float16")
        _buf("wo%d_%d" % (_t, _c), 2 * LC, "float16")
        _buf("s%d_%d" % (_t, _c), LC, "bfloat16")
        _buf("so%d_%d" % (_t, _c), LC, "bfloat16")
        _buf("ac%d_%d" % (_t, _c), 8, "float32")
    _buf("gb%d" % _c, CA + 16, "bfloat16")
    for _n in ("kb", "zb", "fl", "cg", "hb"):
        _buf("%s%d" % (_n, _c), CA, "bfloat16")
    for _n in ("e15", "k15", "t15", "val", "h8", "ov", "X", "zx", "nx", "hx", "w8", "f1", "T", "D", "pw", "pv", "eq", "M",
               "insi", "nin", "xi", "ret", "qe", "go", "fm", "rb", "ar", "eo", "ne", "cl", "hh", "ng"):
        _buf("%s_%d" % (_n, _c), LC, "bfloat16")
    for _n in ("ds", "cf", "mc", "iv", "iq"):
        _buf("%s_%d" % (_n, _c), LC, "float16")
    for _n in ("a1", "a2", "m0", "m1", "m2", "m3", "wb", "fi", "xq"):
        _buf("%s_%d" % (_n, _c), 2 * LC, "float16")
    for _n in ("f4", "y7", "pr", "sh", "sm", "ci", "ri", "mk", "eh"):
        _buf("%s_%d" % (_n, _c), LC, "int32")
    for _n in ("tj", "sx", "tb"):
        _buf("%s_%d" % (_n, _c), LC, "float32")
    for _n in ("off", "c16"):
        _buf("%s_%d" % (_n, _c), LC, "uint16")
    _buf("xl_%d" % _c, 2 * NJ, "uint16")
    _buf("vl_%d" % _c, NJ, "uint16")
    for _n in ("ui", "uj", "uk", "vb"):
        _buf("%s_%d" % (_n, _c), NJ, "int32")
for _i in range(8):
    _buf("p%d" % _i, 512, "float32", "psum")


def overlap(a, b):
    if a[0] != b[0] or a[1] >= b[2] or b[1] >= a[2]:
        return False
    if a[3] == b[3] and a[3] > 1 and (a[1] - b[1]) % a[3]:
        return False
    if a[4] is not None and b[4] is not None and a[4] != b[4]:
        return False
    return True


def rank_program(g, core, T, topo):
    rank = T.rank_of(core)
    if rank is None:
        return
    nxt = T.cores[(rank + 1) % len(T.cores)]
    ops = []
    acc = {}
    Q = {"v": g.vector, "a": g.scalar, "t": g.tensor, "g": g, "s": g.sync}
    QS = {"v": "qv", "a": "qa", "t": "qt", "g": "qg"}
    dn = [0]
    PH = ["set"]
    PS = set("p%d" % i for i in range(8))

    def R(name, a=None, b=None, st=1, p=None):
        n = LOG[name][1] if name in LOG else T[name].shape[1]
        return (name, 0 if a is None else a, n if b is None else b, st, p)

    def ap(r):
        t, o = (LOG[r[0]][3], LOG[r[0]][4]) if r[0] in LOG else (r[0], 0)
        if r[4] is not None:
            return T[t][r[4][0]:r[4][1]:r[4][2], o + r[1]:o + r[2]]
        if r[3] > 1:
            return T[t][:, o + r[1]:o + r[2]:r[3]]
        return T[t][:, o + r[1]:o + r[2]]

    def ind(win, off):
        return ("IND", win, off)

    def x(r):
        if isinstance(r, tuple):
            if r[0] == "IND":
                return ap(r[1]).indirect(ap(r[2]))
            return ap(r)
        return r

    def n_of(r):
        return -(-(r[2] - r[1]) // r[3])

    def add(q, fns, reads, writes, cost, kind="c", lat=0.0, sem=None, inc=0, extra=()):
        i = len(ops)
        rd = []
        for r in reads:
            if isinstance(r, tuple):
                rd += [r[1], r[2]] if r[0] == "IND" else [r]
        wr = []
        for r in writes:
            if r[0] == "IND":
                wr.append(r[1])
                rd.append(r[2])
            else:
                wr.append(r)
        deps = set(extra)
        for lst, isw in ((rd, False), (wr, True)):
            for r in lst:
                ps = r[0] in PS
                for (j, r2, w2) in acc.get(r[0], ()):
                    if ps and ops[j]["q"] != q:
                        deps.add(j)
                    elif (isw or w2) and overlap(r, r2):
                        deps.add(j)
        for lst, isw in ((rd, False), (wr, True)):
            for r in lst:
                cur = acc.setdefault(r[0], [])
                if isw and r[3] == 1 and r[4] is None and r[0] not in PS:
                    cur[:] = [e for e in cur if not (e[1][1] >= r[1] and e[1][2] <= r[2])]
                cur.append((i, r, isw))
        ops.append({"ph": PH[0], "q": q, "fns": fns, "deps": deps, "cost": cost, "kind": kind, "lat": lat, "sem": sem, "inc": inc})
        return i

    def two(*rs):
        return all(isinstance(r, tuple) and r[0] in LOG and LOG[r[0]][2] in ("bfloat16", "float16", "uint16") and r[0] not in PS for r in rs)

    CY = 0.00083

    def vc(n, rate):
        return 0.02 + max(64, n * rate) * CY

    def tt(out, a, b, op):
        rate = 1.6 if a[0] == "IND" else (1.0 if a[0] in PS or b[0] in PS else 2.0)
        return add("v", [lambda: g.vector.tensor_tensor(x(out), x(a), x(b), op)], [a, b], [out], vc(n_of(out), rate))

    def ts(out, a, s1, op0, s2=None, op1=None):
        rate = 0.5 if two(out, a) else 1.0
        if op1 is None:
            f = lambda: g.vector.tensor_scalar(x(out), x(a), x(s1), None, op0)
        else:
            f = lambda: g.vector.tensor_scalar(x(out), x(a), x(s1), x(s2), op0, op1)
        return add("v", [f], [a, s1, s2], [out], vc(n_of(out), rate))

    def cp(out, a):
        rate = 4.0 if out[0] == "IND" else (0.5 if two(out, a) else 1.0)
        return add("v", [lambda: g.vector.tensor_copy(x(out), x(a))], [a], [out], vc(n_of(a), rate))

    def fill(out, v):
        add("v", [lambda: g.vector.memset(x(out), v)], [], [out], 0.1)

    def scan(out, d0, d1):
        add("v", [lambda: g.vector.tensor_tensor_scan(x(out), x(d0), x(d1), 0.0, A.mult, A.add)], [d0, d1], [out], vc(n_of(out), 0.5))

    def act(out, a, func, bias=None, scale=None, accum=None):
        kw = {}
        if func == F.Copy and (bias is not None or scale is not None):
            func = F.Identity
        if bias is not None:
            kw["bias"] = bias
        if scale is not None:
            kw["scale"] = scale
        if accum is not None:
            kw["accum_out"] = accum
        rate = 1.6 if a[0] == "IND" else 1.0
        return add("a", [lambda: g.scalar.activation(x(out), x(a), func, **{k: x(v) for k, v in kw.items()})], [a, bias, scale],
                   [out] + ([accum] if accum is not None else []), 0.04 + max(64, n_of(out) * rate) * CY)

    def mm(items):
        fns, rd, wr, cost = [], [], [], 0.02
        for (o, l, r, s, e) in items:
            fns.append(lambda o=o, l=l, r=r, s=s, e=e: g.tensor.matmul(x(o), x(l), x(r), s, e))
            rd += [l, r]
            wr.append(o)
            cost += max(64, n_of(r)) * CY * (4 if LOG[r[0]][2] == "float32" else 1)
        return add("t", fns, list(dict.fromkeys(rd)), list(dict.fromkeys(wr)), cost)

    def dma(q, out, a):
        s = "d%d" % dn[0]
        dn[0] += 1
        return add(q, [lambda: Q[q].dma_start(x(out), x(a))], [a], [out], 0.1, "d", 2.2, s, 16)

    def remote(tag, out, a):
        m, ne = 0, 8
        for e in topo.engines(core, nxt)[:ne]:
            m |= 1 << e
        rid, pid = topo.addr(nxt)[0], topo.addr(nxt)[1]
        ra, la = T.sem["a" + tag], T.sem["l" + tag]
        i = add("g", [lambda: g.remote_dma(ap(out), ap(a), ra, la, pid, rid, m)], [a], [], 1.2, "r", 2.5, "l" + tag, ne)
        return add("x", [], [], [out], 0.0, "x", 0.0, "a" + tag, ne, (i,))

    ring = [[0] for _ in range(NCH)]

    def bank(c):
        i = ring[c][0]
        ring[c][0] = (i + 1) % (NB - 2)
        return "p%d" % (c * NB + i)

    def nbank(c):
        return "p%d" % (c * NB + NB - 2)

    def wbank(c):
        return "p%d" % (c * NB + NB - 1)

    def lanes(q, buf, name, r0, r1):
        for r in range(r0, r1):
            dma(q, R(buf, 16 * r, 16 * r + 16), R(name, None, None, 1, (r, 128, 16)))
    for j in range(4):
        dma("s", R("er", 1024 * j, 1024 * j + 1024), R("eff", 1024 * j, 1024 * j + 1024))
    lanes("a", "actk", "act", 0, 16 // NCH)
    dma("a", R("sti"), R("st0"))
    for j in range(4):
        dma("s", R("tq", 1024 * j, 1024 * j + 1024), R("req", 1024 * j, 1024 * j + 1024))
    lanes("s", "actk", "act", 16 // NCH, 16)
    fill(R("bari"), 0)
    dma("s", R("bari", None, None, 1, (0, 128, 16)), R("bar"))
    lanes("s", "whyk", "why", 0, 16)

    def iota(out, pattern, base, cm):
        add("g", [lambda: g.iota(x(out), pattern, base, cm)], [], [out], 0.13 + 2 * n_of(out) * CY)
    iota(R("ip"), [[0, 128]], 0, 1)
    iota(R("ic"), [[1, 128]], 0, 0)
    iota(R("xbi"), [[256, NJ]], 0, 0)
    for c in range(NCH):
        iota(R("vb_%d" % c), [[16, NJ]], LC * c, 0)
    ts(R("gp"), R("ip"), 4, A.arith_shift_right)
    ts(R("gc"), R("ic"), 4, A.arith_shift_right)
    ts(R("kp"), R("ip"), 15, A.bitwise_and)
    ts(R("kc"), R("ic"), 15, A.bitwise_and)
    tt(R("blk"), R("gp"), R("gc"), A.is_equal)
    ts(R("ns"), R("blk"), -64.0, A.mult, 64.0, A.add)
    tt(R("cc"), R("kc"), R("ns"), A.add)
    tt(R("pp"), R("kp"), R("ns"), A.add)
    tt(R("dd"), R("kc"), R("pp"), A.subtract)
    ts(R("eye"), R("dd"), 0.0, A.is_equal)
    ts(R("str"), R("dd"), 1.0, A.is_ge)
    ts(R("tri"), R("dd"), 0.0, A.is_ge)
    for nm, de in (("shd", 1.0), ("sh1", -1.0), ("sh2", -2.0), ("sh4", -4.0), ("sh8", -8.0)):
        ts(R("hb0", 0, 128), R("dd"), de, A.is_equal)
        tt(R(nm), R("hb0", 0, 128), R("eye"), A.subtract)
    for nm, f in (("neg", -1.0), ("i4", 4.0), ("im85", -8.5), ("i512", -512.0), ("i71", 71.5), ("i72", 72.0), ("i2048", 2048.0)):
        act(R(nm), R("eye"), F.Copy, None, f)
    ts(R("mt"), R("str"), -32.0, A.mult)
    tt(R("first"), R("mt"), R("eye"), A.add)
    ts(R("half"), R("first"), 0.5, A.mult)
    ts(R("mr"), R("eye"), -64.0, A.mult)
    tt(R("mr"), R("mr"), R("str"), A.add)
    ts(R("e0"), R("pp"), 0.0, A.is_equal)
    ts(R("mt"), R("sh1"), -2.0, A.mult)
    tt(R("mt"), R("mt"), R("e0"), A.subtract)
    ts(R("thf"), R("dd"), 5.0, A.min, 8.0 * LN2, A.mult)
    ts(R("kcol", 0, 1), R("kp", 0, 1), 1.0, A.mult)
    BC = {}
    for q, (nm, v) in enumerate((("thj", 56.0 * LN2 + math.log(0.7)), ("w8", 60.0 * LN2), ("tb", 40.0 * LN2 + math.log(0.7 / 24.0)),
                                 ("f4", -3.5), ("one", -1.0), ("hi", -11.5), ("pv", -40.0 * LN2))):
        BC[nm] = R("m1c", q, q + 1)
        fill(BC[nm], v)
    act(R("mth"), R("thf"), F.Exp, BC["thj"])
    ts(R("blkz"), R("blk"), 1.0 / 24.0, A.mult)
    ts(R("blk4"), R("blk"), 4.0, A.mult)
    ts(R("nblk"), R("blk"), -1.0, A.mult)
    for k in range(16):
        ts(R("wk", 128 * k, 128 * k + 128), R("cc"), float(k), A.is_equal)
    ts(R("kap", 0, 1), R("kcol", 0, 1), 241.0, A.mult, 101.0, A.add)
    for t in range(VI):
        ts(R("kap", 4 + t, 5 + t), R("kap", 0, 1), 2048.0, A.mult, float(97 * t), A.add)
    ts(R("cq", 0, 1), R("kcol", 0, 1), -16.0, A.mult, 0.5, A.add)
    ts(R("k16", 0, 1), R("kcol", 0, 1), -1.0, A.mult, 16.0, A.add)
    fill(R("thr", 0, 1), -1.5)
    fill(R("ones"), 1.0)
    fill(R("allo"), 1.0 / 16.0)
    ts(R("kcol", 2, 3), R("kcol", 0, 1), 16.0, A.mult)
    ts(R("xbase", 0, NJ), R("xbi"), R("kcol", 2, 3), A.add)
    fill(R("xbase", NJ, 2 * NJ), 2048.0)
    ts(R("kcol", 4, 5), R("kcol", 0, 1), 256.0, A.mult)
    for c in range(NCH):
        ts(R("vb_%d" % c), R("vb_%d" % c), R("kcol", 4, 5), A.add)
    cp(R("barb"), R("bari"))
    b = bank(0)
    mm([(R(b, 0, 256), R("e0"), R("barb"), True, True)])
    cp(R("bark"), R(b, 0, 256))
    for c in range(NCH):
        a0, a1 = c * LC, (c + 1) * LC
        ts(R("w0_%d" % c, 0, LC), R("actk", a0, a1), -2048.0, A.add)
        ts(R("w0_%d" % c, LC, 2 * LC), R("whyk", a0, a1), -2047.0, A.add)
    ts(R("sth"), R("sti"), 8.0, A.is_ge, 144.0, A.mult)
    tt(R("stc"), R("sti"), R("sth"), A.add)
    for r in range(16):
        c, o = divmod(16 * r, LC)
        act(R("s0_%d" % c, o, o + 16), R("stc", r, 256, 16), F.Copy, -20.0)

    def code(dst, src, cl, hh, b, n):
        ts(cl, src, 4.0, A.max, 11.0, A.min)
        act(hh, src, F.Sign, BC["hi"])
        mm([(R(b, 0, n), R("eye"), src, True, False), (R(b, 0, n), R("neg"), cl, False, False), (R(b, 0, n), R("i71"), hh, False, True)])
        act(dst, R(b, 0, n), F.Copy, 63.5)
    for j in range(8):
        c0, c1 = 512 * j, 512 * j + 512
        d = 512 * (j % 4)
        if j >= 8 - ND:
            n1, n2 = R("fl%d" % (j % 2), d, d + 512), R("cg%d" % (j % 2), d, d + 512)
            ts(n1, R("er", c0, c1), 4.0, A.max, 11.0, A.min)
            tt(n2, R("er", c0, c1), n1, A.subtract)
            ts(n1, R("er", c0, c1), 12.0, A.is_ge, 143.0, A.mult)
            tt(n2, n2, n1, A.add)
            ts(R("gt", c0, c1), n2, -8.0, A.add)
            continue
        code(R("gt", c0, c1), R("er", c0, c1), R("kb%d" % (j // 4), d, d + 512), R("zb%d" % (j // 4), d, d + 512), bank(j % 2), 512)
    for j in range(4):
        c0, c1 = 1024 * j, 1024 * j + 1024
        ts(R("nt", c0, c1), R("tq", c0, c1), 12.0, A.is_lt, -BIG, A.mult)

    def run(t, c):
        def K(n, *a):
            return R("%s_%d" % (n, c), *a)
        PH[0] = "run%d" % c
        gb, kb, zb, fl = "gb%d" % c, "kb%d" % c, "zb%d" % c, "fl%d" % c
        w, s = "w%d_%d" % (t, c), "s%d_%d" % (t, c)
        ts(K("off"), R(w, 0, LC), 2048.0, A.add)
        b = bank(c)
        for p in range(NP):
            l0, l1 = p * LC // NP, (p + 1) * LC // NP
            e0, e1 = 16 * l0, 16 * l1
            act(R(gb, e0 + 1, e1 + 1), ind(R("gt"), K("off", l0, l1)), F.Copy)
            act(K("e15", l0, l1), R(gb, e0 + 16, e1 + 1, 16), F.Copy, 4.0)
            act(R(gb, e0, e1, 16), R(s, l0, l1), F.Copy)
            ts(R(kb, e0, e1), R(gb, e0, e1), -8.0, A.is_equal)
            scan(R(zb, e0, e1), R(kb, e0, e1), R(gb, e0, e1))
            tt(R(fl, e0, e1), ind(R("nt"), K("off", l0, l1)), R(zb, e0, e1), A.is_gt)
            mm([(R(b, l0, l1), R("wk", 128 * k, 128 * k + 128), R(fl, e0 + k, e1, 16), k == 0, k == 15) for k in range(16)])
        act(K("ov"), R(b, 0, LC), F.Sign, R("thr", 0, 1))
        PH[0] = "end%d" % c
        nb = nbank(c)
        o = R(nb, 0, LC)
        ts(K("k15"), K("e15"), -4.0, A.is_equal)
        tt(K("t15"), K("k15"), R(zb, 15, CA, 16), A.mult)
        mm([(o, R("eye"), K("t15"), True, False), (o, R("eye"), K("e15"), False, True)])
        cp(K("f4"), o)
        act(K("h8"), o, F.Sign, BC["f4"])
        ts(K("y7"), K("f4"), 7, A.bitwise_and)
        mm([(o, R("i4"), K("h8"), True, False), (o, R("i4"), R("ones", 0, LC), False, True)])
        tt(K("val"), K("y7"), o, A.add)
        if t < VI - 1:
            mm([(o, R("eye"), K("val"), True, False), (o, R("i72"), K("h8"), False, True)])
            act(R("so%d_%d" % (t, c)), o, F.Copy, 52.0)
            remote("s%d_%d" % (t, c), R("s%d_%d" % (t + 1, c)), R("so%d_%d" % (t, c)))
        o = R(nb, 0, NJ)
        mm([(o, R("wk", 128 * r, 128 * r + 128), R("val_%d" % c, r, LC, 16), r == 0, r == 15) for r in range(16)])
        cp(K("ui"), o)
        ts(K("uj"), K("ui"), 15, A.bitwise_and)
        tt(K("uk"), K("uj"), K("vb"), A.add)
        cp(K("vl"), K("uk"))
        act(K("eo"), ind(R("er"), K("vl")), F.Copy)
        o = R(nb, 0, LC)
        mm([(o, R("eye"), K("eo"), True, False), (o, R("eye"), K("val"), False, True)])
        ts(K("eh"), o, 0.5, A.mult, -0.25, A.add)
        cp(K("ne"), K("eh"))
        if t < VI - 1:
            code(K("ng"), K("ne"), K("cl"), K("hh"), nb, LC)
        cp(ind(R("er"), K("vl")), K("ne"))

    def table(t, c):
        PH[0] = "tab"
        if t < VI - 1:
            cp(ind(R("gt"), R("vl_%d" % c)), R("ng_%d" % c))

    def cand(t, c):
        def K(n, *a):
            return R("%s_%d" % (n, c), *a)
        PH[0] = "head%d" % c
        w = "w%d_%d" % (t, c)
        S_, Q_ = R(w, 0, LC), R(w, LC, 2 * LC)
        pw, nb = wbank(c), nbank(c)
        wp, n2 = R(pw, 0, 2 * LC), R(nb, 0, 2 * LC)
        mm([(wp, R("eye"), R(w, 0, 2 * LC), True, True)])
        wS = R(pw, 0, LC)
        b = bank(c)
        mm([(R(b, 0, LC), R("half"), K("ov"), True, True)])
        act(K("X"), R(b, 0, LC), F.Relu, R("cq", 0, 1))
        ts(K("xq", 0, LC), K("X"), R("kcol", 0, 1), A.mult)
        tt(K("xq", LC, 2 * LC), K("X"), wS, A.mult)
        b = bank(c)
        mm([(R(b, 0, 2 * NJ), R("wk", 128 * r, 128 * r + 128), R("xq_%d" % c, r, 2 * LC, 16), r == 0, False) for r in range(16)]
           + [(R(b, 0, 2 * NJ), R("eye"), R("xbase"), False, True)])
        cp(K("xl"), R(b, 0, 2 * NJ))
        b = bank(c)
        mm([(R(b, 0, LC), R("mth"), K("X"), True, True)])
        act(K("tj"), R(b, 0, LC), F.Copy)
        act(K("zx"), ind(R("zb%d" % c), K("xl", 0, NJ)), F.Copy)
        act(K("nx"), ind(R("nt"), K("xl", NJ, 2 * NJ)), F.Copy)
        ts(K("hx"), K("zx"), 0.0, A.is_ge)
        b = bank(c)
        mm([(R(b, 0, LC), R("eye"), K("zx"), True, False), (R(b, 0, LC), R("i512"), K("hx"), False, False), (R(b, 0, LC), R("eye"), K("nx"), False, True)])
        act(K("w8"), R(b, 0, LC), F.Exp, BC["w8"], LN2)
        ts(K("f1"), K("w8"), 0.0, A.is_gt)
        b = bank(c)
        mm([(R(b, 0, LC), R("blk"), K("w8"), True, True)])
        tt(K("T"), R(b, 0, LC), K("tj"), A.is_ge)
        b = bank(c)
        mm([(R(b, 0, LC), R("mt"), K("T"), True, False), (R(b, 0, LC), R("eye"), K("X"), False, True)])
        act(K("D"), R(b, 0, LC), F.Relu)
        tt(K("ds"), K("D"), wS, A.mult)
        b = bank(c)
        mm([(R(b, 0, LC), R("blk"), K("xq", LC, 2 * LC), True, True)])
        mm([(R(b, LC, 2 * LC), R("blk"), K("ds"), True, True)])
        mm([(R(pw, 2 * LC, 3 * LC), R("blk"), K("ds"), True, False), (R(pw, 2 * LC, 3 * LC), R("eye"), R("ones", 0, LC), False, True)])
        act(K("sx"), R(b, 0, LC), F.Copy, 2048.0)
        act(R(b, 2 * LC, 3 * LC), R(b, 0, LC), F.Copy, R("kap", 4 + t, 5 + t), R("kap", 0, 1))
        tt(K("pr"), R(b, LC, 2 * LC), K("sx"), A.mult)
        ts(K("sh"), K("pr"), 5, A.arith_shift_right)
        tt(K("sm"), K("sh"), R(b, 2 * LC, 3 * LC), A.add)
        ts(K("ci"), K("sm"), 4095, A.bitwise_and)
        cp(K("c16"), K("ci"))
        PH[0] = "net%d" % c

        def prod(n, wd, mask):
            tt(K(n, 0, LC), R(wd[0], wd[1], wd[1] + LC), mask, A.mult)
            tt(K(n, LC, 2 * LC), R(wd[0], wd[1] + LC, wd[1] + 2 * LC), mask, A.mult)
        ts(K("cf"), K("ci"), -2048.0, A.add)
        tt(K("qe"), Q_, R(pw, 2 * LC, 3 * LC), A.is_equal)
        o = R(nb, 0, LC)
        mm([(o, R("eye"), K("D"), True, False), (o, R("eye"), K("qe"), False, False), (o, R("blk4"), K("X"), False, True)])
        ts(K("go"), o, 4.5, A.is_ge)
        pr = R(nb, LC, 2 * LC)
        mm([(o, R("blk"), K("go"), True, True), (pr, R("mr"), K("go"), True, True)])
        act(K("rb"), pr, F.Relu)
        ts(K("fm"), o, R("k16", 0, 1), A.is_ge)
        o2 = R(nb, 2 * LC, 3 * LC)
        mm([(o2, R("tri"), K("X"), True, True)])
        tt(K("a1", 0, LC), S_, o2, A.mult)
        tt(K("a1", LC, 2 * LC), Q_, o2, A.mult)
        tt(K("iq"), K("X"), R(pw, 2 * LC, 3 * LC), A.mult)
        prod("a2", wp, K("go"))
        tt(K("fi", 0, LC), K("fm"), K("cf"), A.mult)
        ts(K("fi", LC, 2 * LC), K("fm"), -2048.0, A.mult)
        base, moves = R(w, 0, 2 * LC), [("neg", "a2")]
        for s in range(4):
            ts(K("ri"), pr, 0.0, A.max)
            ts(K("mk"), K("ri"), s, A.arith_shift_right, 1, A.bitwise_and)
            prod("m%d" % s, wp, K("mk"))
            moves.append(("sh%d" % (1 << s), "m%d" % s))
            if s < 3:
                tt(K("ar"), pr, K("mk"), A.mult)
                pr = R(nb, ((s + 2) % 4) * LC, ((s + 2) % 4 + 1) * LC)
                mm([(pr, R("eye"), K("rb"), True, False), (pr, R("sh%d" % (1 << s)), K("ar"), False, True)])
                if s < 2:
                    act(K("rb"), pr, F.Copy)
            if s == 3:
                moves += [("eye", "fi")]
            mm([(wp, R("eye"), base, True, False)] + [(wp, R(m), K(a), False, q == len(moves) - 1) for q, (m, a) in enumerate(moves)])
            if s == 1:
                cp(K("wb"), wp)
                base, moves = K("wb"), []
        mm([(n2, R("eye"), R(w, 0, 2 * LC), True, False), (n2, R("shd"), K("a1"), False, False),
            (R(nb, LC, 2 * LC), R("eye"), K("iq"), False, True)])
        PH[0] = "score%d" % c
        hb, cg = "hb%d" % c, "cg%d" % c
        rb_ = bank(c)
        rr = R(rb_, 0, LC)
        mm([(rr, R("im85"), K("hx"), True, False), (rr, R("eye"), K("nx"), False, True)])
        b = bank(c)
        mm([(R(b, 0, LC), R("nblk"), K("f1"), True, False), (R(b, 0, LC), R("eye"), R("bark", c * LC, (c + 1) * LC), False, True)])
        act(K("tb"), R(b, 0, LC), F.Exp, BC["tb"], 5.0 * LN2)
        act(R(cg), ind(R("gt"), K("c16")), F.Copy)
        for m in range(16):
            tt(R(hb, m * LC, (m + 1) * LC), R(cg, m, CA, 16), rr, A.is_gt)
        mm([(R(b, m, 128, 16), R(hb, m * LC, (m + 1) * LC), R("blk", 0, 128, 16), True, True) for m in range(16)])
        act(K("pv"), R(b, 0, LC), F.Exp, BC["pv"], 5.0 * LN2)
        mm([(R(b, LC, 2 * LC), K("pv"), R("eye"), True, True)])
        act(K("pw"), R(b, LC, 2 * LC), F.Copy)
        mm([(rr, R("blkz"), K("pw"), True, True)])
        tt(K("eq"), rr, K("pw"), A.is_le)
        tt(K("insi"), rr, K("tb"), A.is_ge)
        tt(K("nin"), rr, K("tb"), A.is_lt)
        b = bank(c)
        mm([(R(b, 0, LC), R("first"), K("eq"), True, True)])
        act(K("M"), R(b, 0, LC), F.Relu)
        mm([(R(b, 2 * LC, 3 * LC), R("eye"), K("X"), True, False), (R(b, 2 * LC, 3 * LC), R("eye"), K("insi"), False, True),
            (R(b, 3 * LC, 4 * LC), R("blk"), K("X"), True, False), (R(b, 3 * LC, 4 * LC), R("neg"), K("insi"), False, True)])
        act(K("xi"), R(b, 2 * LC, 3 * LC), F.Relu, BC["one"])
        if t < VI - 1:
            act(K("ret"), R(b, 3 * LC, 4 * LC), F.Relu, accum=R("ac%d_%d" % (t, c), 0, 1))
        tt(K("mc"), K("M"), K("cf"), A.mult)
        mm([(rr, R("blk"), K("mc"), True, True)])
        PH[0] = "fin%d" % c
        prod("m0", n2, K("insi"))
        prod("m1", wp, K("nin"))
        tt(K("iv"), K("xi"), rr, A.mult)
        b = bank(c)
        fp = R(b, 0, 2 * LC)
        mm([(fp, R("eye"), K("m1"), True, False), (fp, R("eye"), K("m0"), False, False), (R(b, 0, LC), R("eye"), K("iv"), False, True)])
        if t < VI - 1:
            wo = "wo%d_%d" % (t, c)
            cp(R(wo), fp)
            remote("p%d_%d" % (t, c), R("w%d_%d" % (t + 1, c)), R(wo))
        else:
            act(R("ysk", c * LC, (c + 1) * LC), R(b, 0, LC), F.Copy, 2048.0)
            act(R("ywk", c * LC, (c + 1) * LC), R(b, LC, 2 * LC), F.Copy, 2047.0)
            for r in range(c * NJ, (c + 1) * NJ):
                dma("s", R("ys", None, None, 1, (r, 128, 16)), R("ysk", 16 * r, 16 * r + 16))
                dma("a" if c == NCH - 1 else "s", R("yw", None, None, 1, (r, 128, 16)), R("ywk", 16 * r, 16 * r + 16))

    def count(t):
        b = bank(0)
        mm([(R(b, 0, 1), R("allo"), R("ac%d_%d" % (t, c), 0, 1), c == 0, c == NCH - 1) for c in range(NCH)])
        cp(R("rci", 0, 1), R(b, 0, 1))
        ts(R("rci", 4, 5), R("rci", 0, 1), 1, A.bitwise_and)
        ts(R("thr", 0, 1), R("rci", 4, 5), -1.0, A.mult, -1.5, A.add)

    for t in range(VI):
        for c in range(NCH):
            run(t, c)
        for c in range(NCH):
            cand(t, c)
        for c in range(NCH):
            table(t, c)
        if t < VI - 1:
            count(t)
    for j in range(2):
        dma("s" if j else "a", R("ye", 2048 * j, 2048 * j + 2048), R("er", 2048 * j, 2048 * j + 2048))

    n = len(ops)
    HOP = 0.07
    tail = [0.0] * n
    succ = [[] for _ in range(n)]
    for i, o in enumerate(ops):
        for d in o["deps"]:
            succ[d].append(i)
    for i in range(n - 1, -1, -1):
        o = ops[i]
        m = 0.0
        for j in succ[i]:
            m = max(m, tail[j])
        tail[i] = m + o["cost"] + o["lat"] + HOP
    prio = [tail[i] + BIAS.get(ops[i]["ph"], 0.0) for i in range(n)]
    ndep = [len(o["deps"]) for o in ops]
    ready = [0.0] * n
    avail = [i for i in range(n) if ndep[i] == 0]
    free = {q: 0.0 for q in "vatgsx"}
    order = []
    while avail:
        best = None
        for i in avail:
            q = ops[i]["q"]
            st = ready[i] if q == "x" else max(ready[i], free[q])
            key = (round(st, 2), -prio[i], i)
            if best is None or key < best[0]:
                best = (key, i, st)
        _, i, st = best
        avail.remove(i)
        o = ops[i]
        if o["q"] != "x":
            free[o["q"]] = st + o["cost"]
        fin = st + o["cost"] + o["lat"]
        order.append(i)
        for j in succ[i]:
            ready[j] = max(ready[j], fin + (HOP if ops[j]["q"] != o["q"] else 0.03))
            ndep[j] -= 1
            if ndep[j] == 0:
                avail.append(j)

    cnt = {"qv": 0, "qa": 0, "qt": 0, "qg": 0}
    known = {q: {} for q in "vatgs"}
    done = {}
    tot = {}

    def wait(q, sem, v):
        if known[q].get(sem, 0) < v:
            Q[q].wait_ge(T.sem[sem], v)
            known[q][sem] = v

    for i in order:
        o = ops[i]
        q = o["q"]
        if q == "x":
            done[i] = (o["sem"], o["inc"], {o["sem"]: o["inc"]})
            tot[o["sem"]] = o["inc"]
            continue
        for d in sorted(o["deps"], reverse=True):
            sem, v, clk = done[d]
            if known[q].get(sem, 0) < v:
                wait(q, sem, v)
                for s2, v2 in clk.items():
                    if known[q].get(s2, 0) < v2:
                        known[q][s2] = v2
        for f in o["fns"]:
            r = f()
            if o["kind"] == "c":
                cnt[QS[q]] += 1
                r.then_inc(T.sem[QS[q]], 1)
            elif o["kind"] == "d":
                r.then_inc(T.sem[o["sem"]], 16)
        clk = dict(known[q])
        s, v = (QS[q], cnt[QS[q]]) if o["kind"] == "c" else (o["sem"], o["inc"])
        clk[s] = v
        done[i] = (s, v, clk)
        tot[s] = v
    for s, v in tot.items():
        wait("g", s, v)
